import numpy as np
import ml_dtypes


def mxq(x, axis, fmt="e4m3"):
    dtype, down = {"e4m3": (ml_dtypes.float8_e4m3fn, 7), "e5m2": (ml_dtypes.float8_e5m2, 14)}[fmt]
    v = np.moveaxis(np.asarray(x, np.float32).astype(ml_dtypes.bfloat16).astype(np.float64), axis, -1)
    blocks = v.reshape(v.shape[:-1] + (-1, 32))
    amax = np.abs(blocks).max(-1, keepdims=True)
    byte = np.maximum(np.where(amax > 0, np.frexp(amax)[1] - 1 + 127, 0) - down, 1)
    scale = np.exp2(byte - 127.0)
    codes = (blocks / scale).astype(np.float32).astype(dtype).astype(np.float64)
    return np.moveaxis((codes * scale).reshape(v.shape), -1, axis)


WIDE = False


def mx_kscale(k):
    if not WIDE:
        return np.ones(k)
    levels = np.array([10, -10, 5, -5, 0])
    if k % 512:
        return np.exp2(np.random.permutation(np.resize(levels, k // 32))).repeat(32)
    a = np.empty((k // 512, 16))
    for p in range(k // 512):
        a[p, :8] = np.random.permutation(np.resize(levels, 8))
        for g in range(8):
            far = levels[np.abs(levels - a[p, g]) >= 10]
            a[p, g + 8] = far[np.random.randint(len(far))]
    return np.exp2(a.ravel()).repeat(32)


def f64(x):
    return np.asarray(x).astype(np.float64)


def striped(idx):
    return np.tile(idx.reshape(-1, 16).T, (8, 1)).astype(np.uint16)


def unstriped(offs):
    return offs[:16].T.reshape(-1).astype(np.int64)


def pack_weight(w):
    k, n = w.shape
    w = f64(np.asarray(w, np.float32).astype(ml_dtypes.bfloat16)).reshape(k // 32, 32, n)
    amax = np.abs(w).max(1)
    byte = np.clip(np.where(amax > 0, np.frexp(amax)[1] - 1 + 127 - 7, 1), 1, 254)
    scaled = (w * np.exp2(127.0 - byte)[:, None, :]).reshape(k, n).astype(np.float32)
    words = np.ascontiguousarray(scaled.reshape(k // 512, 128, 4, n).transpose(0, 1, 3, 2)).astype(ml_dtypes.float8_e4m3fn).view(np.uint8)
    return words, np.ascontiguousarray(byte.astype(np.uint8).reshape(k // 512, 16, n))


def unpack_weight(words, scales):
    g, p, n, _ = words.shape
    vals = np.ascontiguousarray(words).view(ml_dtypes.float8_e4m3fn).astype(np.float64) * np.repeat(np.exp2(scales.astype(np.float64) - 127.0), 8, axis=1)[..., None]
    return vals.transpose(0, 1, 3, 2).reshape(g * 512, n)


def relu(v):
    return np.maximum(v, 0.0)


K, T, S, D, H, V, G = 512, 1024, 512, 2, 512, 1024, 2048


def setup_inputs():
    n = np.random.standard_normal
    s = mx_kscale(K)[:, None]
    u = mx_kscale(H)
    packed_xT = pack_weight(n((K, T)) * s)
    packed_vT = pack_weight(n((H, G)) / np.sqrt(H) / u[:, None])
    return {
        "x_words": packed_xT[0],
        "x_scales": packed_xT[1],
        "w1": (n((K, H)) / np.sqrt(K) / s * u).astype(np.float32),
        "v_words": packed_vT[0],
        "v_scales": packed_vT[1],
        "offs": striped(np.random.permutation(T)[:S]),
        "doc": striped(np.random.permutation(G)[:V]),
    }


def reference(x_words, x_scales, w1, v_words, v_scales, offs, doc):
    xq = unpack_weight(x_words, x_scales)[:, unstriped(offs)]
    h = relu(mxq(f64(w1), 0, "e4m3").T @ xq)
    v_doc = unpack_weight(v_words, v_scales)[:, unstriped(doc)]
    y = mxq(h, 0, "e4m3").T @ v_doc
    return y.reshape(H, S, D).max(axis=2)

@@ -1,0 +1,135 @@
+from contextlib import ExitStack
+
+import concourse.mybir as mybir
+
+K, T, S, D, H, V, G = 512, 1024, 512, 2, 512, 1024, 2048
+FLOPS = 2 * K * H * S + 2 * H * S * V
+
+F32 = mybir.dt.float32
+BF16 = mybir.dt.bfloat16
+I32 = mybir.dt.int32
+U32 = mybir.dt.uint32
+U16 = mybir.dt.uint16
+U8 = mybir.dt.uint8
+FP8X4 = mybir.dt.float8_e4m3fn_x4
+RELU = mybir.ActivationFunctionType.Relu
+COPY = mybir.ActivationFunctionType.Copy
+MAX = mybir.AluOpType.max
+
+P = 128
+PACK = 4
+BANK = 512
+W_CHUNKS = 2
+
+
+def load_scale_rows(queue, window, scales):
+    for q in range(4):
+        queue.dma_start(out=window[32 * q : 32 * q + 4, :].bitcast(I32), in_=scales[0, 4 * q : 4 * q + 4, :].bitcast(I32))
+
+
+def tile_picked_zlateq_relu_p_kernel(tc, x_words, x_scales, w1, v_words, v_scales, offs, doc, out):
+    nc = tc.nc
+    with ExitStack() as ctx:
+        keep = ctx.enter_context(tc.tile_pool(name="keep", bufs=1))
+        psum = ctx.enter_context(tc.psum_pool(name="psum", bufs=8))
+
+        offs_sb = keep.tile([P, S // 16], U16)
+        doc_sb = keep.tile([P, V // 16], U16)
+        xs_win = keep.tile([P, T], U8, align_bytes=64)
+        vs_win = keep.tile([P, G], U8, align_bytes=64)
+        xw_win = keep.tile([P, T], U32, align_bytes=64)
+        vw_win = keep.tile([P, G], U32, align_bytes=64)
+        warm = keep.tile([P, 8], F32)
+        warm_out = keep.tile([P, 8], F32)
+
+        nc.vector.memset(vs_win[:].bitcast(I32), 0)
+        nc.vector.memset(warm[:], 0.0)
+        nc.scalar.activation(warm_out[:], warm[:], RELU)
+
+        nc.sync.dma_start(offs_sb[:], offs)
+        nc.sync.dma_start(doc_sb[:], doc)
+        for q in range(4):
+            rows = x_scales[0, 4 * q : 4 * q + 4, :].bitcast(I32)
+            nc.sync.dma_start(out=xs_win[32 * q : 32 * q + 32, :].bitcast(I32), in_=rows.partition_broadcast(8))
+        nc.sync.dma_start(out=xw_win[:].bitcast(I32), in_=x_words[0].rearrange("p n r -> p (n r)").bitcast(I32))
+        wc = H // W_CHUNKS
+        w_rows = w1.rearrange("(p j) i -> p j i", j=PACK)
+        w_raw = [keep.tile([P, PACK, wc], F32, align_bytes=64, tag="slot%d" % c, name="w_raw%d" % c) for c in range(W_CHUNKS)]
+        for c in range(W_CHUNKS):
+            nc.sync.dma_start(out=w_raw[c][:], in_=w_rows[:, :, c * wc : (c + 1) * wc])
+            if c == 0:
+                load_scale_rows(nc.sync, vs_win, v_scales)
+        nc.sync.dma_start(out=vw_win[:].bitcast(I32), in_=v_words[0].rearrange("p n r -> p (n r)").bitcast(I32))
+
+        xs = keep.tile([P, S], U8, align_bytes=64)
+        xw = keep.tile([P, S], U32, align_bytes=64)
+        nc.vector.tensor_copy(xs[:], xs_win[:].indirect(offs_sb[:]))
+        nc.vector.tensor_copy(xw[:], xw_win[:].indirect(offs_sb[:]))
+
+        halves = V // BANK
+        vs = [keep.tile([P, BANK], U8, align_bytes=64, name="vs%d" % a) for a in range(halves)]
+        doc_cols = [doc_sb[:, a * BANK // 16 : (a + 1) * BANK // 16] for a in range(halves)]
+        for a in range(halves):
+            nc.vector.tensor_copy(vs[a][:], vs_win[:].indirect(doc_cols[a]))
+
+        w_bf = keep.tile([P, H * PACK], BF16, align_bytes=64)
+        w_dst = w_bf[:].rearrange("p (t m j) -> p m j t", t=PACK, j=PACK)
+        mc = wc // PACK
+        for c in range(W_CHUNKS):
+            nc.scalar.activation(w_dst[:, c * mc : (c + 1) * mc], w_raw[c][:].rearrange("p j (m t) -> p m j t", t=PACK), COPY)
+        w_codes = keep.tile([P, H], U32, align_bytes=64)
+        w_scales = keep.tile([P, H], U8, align_bytes=64)
+        nc.vector.quantize_mx(out=w_codes[:].bitcast(FP8X4), scales=w_scales[:], in_=w_bf[:])
+
+        blocks = S // P
+        h_bf = []
+        for b in range(blocks):
+            h_acc = psum.tile([P, BANK], F32, tag="bank", name="h_acc%d" % b)
+            cols = slice(b * P, (b + 1) * P)
+            for t in range(PACK):
+                ch = slice(t * P, (t + 1) * P)
+                nc.tensor.matmul_mx(
+                    out=h_acc[:, ch],
+                    lhsT=w_codes[:, ch].bitcast(FP8X4),
+                    lhsT_scale=w_scales[:, ch],
+                    rhs=xw[:, cols].bitcast(FP8X4),
+                    rhs_scale=xs[:, cols],
+                    start=True,
+                    stop=True,
+                )
+            hb = keep.tile([P, P * PACK], BF16, align_bytes=64, name="h_bf%d" % b)
+            nc.scalar.activation(hb[:].rearrange("p (n t) -> p n t", t=PACK), h_acc[:].rearrange("p (t n) -> p n t", t=PACK), RELU)
+            h_bf.append(hb)
+
+        h_codes = [keep.tile([P, P], U32, align_bytes=64, name="h_codes%d" % b) for b in range(blocks)]
+        h_scales = [keep.tile([P, P], U8, align_bytes=64, name="h_scales%d" % b) for b in range(blocks)]
+
+        def quantise_h(b):
+            nc.vector.quantize_mx(out=h_codes[b][:].bitcast(FP8X4), scales=h_scales[b][:], in_=h_bf[b][:])
+
+        vw_all = keep.tile([P, V], U32, align_bytes=64, tag="slot%d" % (W_CHUNKS - 1))
+        vw = [vw_all[:, a * BANK : (a + 1) * BANK] for a in range(halves)]
+        nc.vector.tensor_copy(vw[0], vw_win[:].indirect(doc_cols[0]))
+        quantise_h(0)
+        nc.vector.tensor_copy(vw[1], vw_win[:].indirect(doc_cols[1]))
+        for b in range(1, blocks):
+            quantise_h(b)
+
+        nv = BANK // D
+        for a in range(halves):
+            for b in range(blocks):
+                y_acc = psum.tile([P, BANK], F32, tag="bank", name="y_acc%d_%d" % (a, b))
+                nc.tensor.matmul_mx(
+                    out=y_acc[:],
+                    lhsT=h_codes[b][:].bitcast(FP8X4),
+                    lhsT_scale=h_scales[b][:],
+                    rhs=vw[a].bitcast(FP8X4),
+                    rhs_scale=vs[a][:],
+                    start=True,
+                    stop=True,
+                )
+                odd = keep.tile([P, nv], F32, name="odd%d_%d" % (a, b))
+                best = keep.tile([P, nv], F32, name="best%d_%d" % (a, b))
+                nc.scalar.activation(odd[:], y_acc[:, 1::2], COPY)
+                nc.vector.tensor_tensor(best[:], y_acc[:, 0::2], odd[:], MAX)
+                nc.sync.dma_start(out=out[b * P : (b + 1) * P, a * nv : (a + 1) * nv], in_=best[:])

@@ -19,12 +19,7 @@ MAX = mybir.AluOpType.max
 P = 128
 PACK = 4
 BANK = 512
-W_CHUNKS = 2
-
-
-def load_scale_rows(queue, window, scales):
-    for q in range(4):
-        queue.dma_start(out=window[32 * q : 32 * q + 4, :].bitcast(I32), in_=scales[0, 4 * q : 4 * q + 4, :].bitcast(I32))
+W_SPLIT = 256
 
 
 def tile_picked_zlateq_relu_p_kernel(tc, x_words, x_scales, w1, v_words, v_scales, offs, doc, out):
@@ -39,50 +34,50 @@ def tile_picked_zlateq_relu_p_kernel(tc, x_words, x_scales, w1, v_words, v_scale
         vs_win = keep.tile([P, G], U8, align_bytes=64)
         xw_win = keep.tile([P, T], U32, align_bytes=64)
         vw_win = keep.tile([P, G], U32, align_bytes=64)
-        warm = keep.tile([P, 8], F32)
+        zero = keep.tile([P, 8], F32)
         warm_out = keep.tile([P, 8], F32)
 
         nc.vector.memset(vs_win[:].bitcast(I32), 0)
-        nc.vector.memset(warm[:], 0.0)
-        nc.scalar.activation(warm_out[:], warm[:], RELU)
+        nc.vector.memset(zero[:], 0.0)
+        nc.scalar.activation(warm_out[:], zero[:], RELU)
 
         nc.sync.dma_start(offs_sb[:], offs)
-        nc.sync.dma_start(doc_sb[:], doc)
         for q in range(4):
             rows = x_scales[0, 4 * q : 4 * q + 4, :].bitcast(I32)
             nc.sync.dma_start(out=xs_win[32 * q : 32 * q + 32, :].bitcast(I32), in_=rows.partition_broadcast(8))
+        nc.sync.dma_start(doc_sb[:], doc)
         nc.sync.dma_start(out=xw_win[:].bitcast(I32), in_=x_words[0].rearrange("p n r -> p (n r)").bitcast(I32))
-        wc = H // W_CHUNKS
         w_rows = w1.rearrange("(p j) i -> p j i", j=PACK)
-        w_raw = [keep.tile([P, PACK, wc], F32, align_bytes=64, tag="slot%d" % c, name="w_raw%d" % c) for c in range(W_CHUNKS)]
-        for c in range(W_CHUNKS):
-            nc.sync.dma_start(out=w_raw[c][:], in_=w_rows[:, :, c * wc : (c + 1) * wc])
-            if c == 0:
-                load_scale_rows(nc.sync, vs_win, v_scales)
+        w_first = keep.tile([P, PACK, W_SPLIT], F32)
+        w_last = keep.tile([P, PACK, H - W_SPLIT], F32, align_bytes=64, tag="after_cast")
+        nc.sync.dma_start(out=w_first[:], in_=w_rows[:, :, :W_SPLIT])
+        for q in range(4):
+            nc.sync.dma_start(out=vs_win[32 * q : 32 * q + 4, :].bitcast(I32), in_=v_scales[0, 4 * q : 4 * q + 4, :].bitcast(I32))
+        nc.sync.dma_start(out=w_last[:], in_=w_rows[:, :, W_SPLIT:])
         nc.sync.dma_start(out=vw_win[:].bitcast(I32), in_=v_words[0].rearrange("p n r -> p (n r)").bitcast(I32))
 
         xs = keep.tile([P, S], U8, align_bytes=64)
         xw = keep.tile([P, S], U32, align_bytes=64)
+        vs = keep.tile([P, V], U8, align_bytes=64)
         nc.vector.tensor_copy(xs[:], xs_win[:].indirect(offs_sb[:]))
         nc.vector.tensor_copy(xw[:], xw_win[:].indirect(offs_sb[:]))
-
-        halves = V // BANK
-        vs = [keep.tile([P, BANK], U8, align_bytes=64, name="vs%d" % a) for a in range(halves)]
-        doc_cols = [doc_sb[:, a * BANK // 16 : (a + 1) * BANK // 16] for a in range(halves)]
-        for a in range(halves):
-            nc.vector.tensor_copy(vs[a][:], vs_win[:].indirect(doc_cols[a]))
+        nc.vector.tensor_copy(vs[:], vs_win[:].indirect(doc_sb[:]))
 
         w_bf = keep.tile([P, H * PACK], BF16, align_bytes=64)
         w_dst = w_bf[:].rearrange("p (t m j) -> p m j t", t=PACK, j=PACK)
-        mc = wc // PACK
-        for c in range(W_CHUNKS):
-            nc.scalar.activation(w_dst[:, c * mc : (c + 1) * mc], w_raw[c][:].rearrange("p j (m t) -> p m j t", t=PACK), COPY)
+        nc.scalar.activation(w_dst[:, : W_SPLIT // PACK], w_first[:].rearrange("p j (m t) -> p m j t", t=PACK), COPY)
+        nc.scalar.activation(w_dst[:, W_SPLIT // PACK :], w_last[:].rearrange("p j (m t) -> p m j t", t=PACK), COPY)
         w_codes = keep.tile([P, H], U32, align_bytes=64)
         w_scales = keep.tile([P, H], U8, align_bytes=64)
         nc.vector.quantize_mx(out=w_codes[:].bitcast(FP8X4), scales=w_scales[:], in_=w_bf[:])
 
+        vw = keep.tile([P, V], U32, align_bytes=64, tag="after_cast")
+        nc.vector.tensor_copy(vw[:, :BANK], vw_win[:].indirect(doc_sb[:, : BANK // 16]))
+        nc.vector.tensor_copy(vw[:, BANK:], vw_win[:].indirect(doc_sb[:, BANK // 16 :]))
+
         blocks = S // P
-        h_bf = []
+        h_codes = []
+        h_scales = []
         for b in range(blocks):
             h_acc = psum.tile([P, BANK], F32, tag="bank", name="h_acc%d" % b)
             cols = slice(b * P, (b + 1) * P)
@@ -97,39 +92,34 @@ def tile_picked_zlateq_relu_p_kernel(tc, x_words, x_scales, w1, v_words, v_scale
                     start=True,
                     stop=True,
                 )
-            hb = keep.tile([P, P * PACK], BF16, align_bytes=64, name="h_bf%d" % b)
-            nc.scalar.activation(hb[:].rearrange("p (n t) -> p n t", t=PACK), h_acc[:].rearrange("p (t n) -> p n t", t=PACK), RELU)
-            h_bf.append(hb)
-
-        h_codes = [keep.tile([P, P], U32, align_bytes=64, name="h_codes%d" % b) for b in range(blocks)]
-        h_scales = [keep.tile([P, P], U8, align_bytes=64, name="h_scales%d" % b) for b in range(blocks)]
-
-        def quantise_h(b):
-            nc.vector.quantize_mx(out=h_codes[b][:].bitcast(FP8X4), scales=h_scales[b][:], in_=h_bf[b][:])
-
-        vw_all = keep.tile([P, V], U32, align_bytes=64, tag="slot%d" % (W_CHUNKS - 1))
-        vw = [vw_all[:, a * BANK : (a + 1) * BANK] for a in range(halves)]
-        nc.vector.tensor_copy(vw[0], vw_win[:].indirect(doc_cols[0]))
-        quantise_h(0)
-        nc.vector.tensor_copy(vw[1], vw_win[:].indirect(doc_cols[1]))
-        for b in range(1, blocks):
-            quantise_h(b)
+            h_bf = keep.tile([P, P * PACK], BF16, align_bytes=64, name="h_bf%d" % b)
+            nc.scalar.activation(
+                h_bf[:].rearrange("p (n t) -> p n t", t=PACK),
+                h_acc[:].rearrange("p (t n) -> p n t", t=PACK),
+                RELU,
+            )
+            h_codes.append(keep.tile([P, P], U32, align_bytes=64, name="h_codes%d" % b))
+            h_scales.append(keep.tile([P, P], U8, align_bytes=64, name="h_scales%d" % b))
+            nc.vector.quantize_mx(out=h_codes[b][:].bitcast(FP8X4), scales=h_scales[b][:], in_=h_bf[:])
 
         nv = BANK // D
-        for a in range(halves):
+        for a in range(V // BANK):
             for b in range(blocks):
                 y_acc = psum.tile([P, BANK], F32, tag="bank", name="y_acc%d_%d" % (a, b))
                 nc.tensor.matmul_mx(
                     out=y_acc[:],
                     lhsT=h_codes[b][:].bitcast(FP8X4),
                     lhsT_scale=h_scales[b][:],
-                    rhs=vw[a].bitcast(FP8X4),
-                    rhs_scale=vs[a][:],
+                    rhs=vw[:, a * BANK : (a + 1) * BANK].bitcast(FP8X4),
+                    rhs_scale=vs[:, a * BANK : (a + 1) * BANK],
                     start=True,
                     stop=True,
                 )
-                odd = keep.tile([P, nv], F32, name="odd%d_%d" % (a, b))
                 best = keep.tile([P, nv], F32, name="best%d_%d" % (a, b))
-                nc.scalar.activation(odd[:], y_acc[:, 1::2], COPY)
-                nc.vector.tensor_tensor(best[:], y_acc[:, 0::2], odd[:], MAX)
+                if blocks * a + b in (0, 3, 6):
+                    nc.vector.tensor_reduce(best[:], y_acc[:].rearrange("p (v d) -> p v d", d=D), mybir.AxisListType.X, MAX)
+                else:
+                    y_sb = keep.tile([P, BANK], F32, name="y_sb%d_%d" % (a, b))
+                    nc.scalar.activation(y_sb[:], y_acc[:], COPY)
+                    nc.vector.tensor_tensor(best[:], y_sb[:, 0::2], y_sb[:, 1::2], MAX)
                 nc.sync.dma_start(out=out[b * P : (b + 1) * P, a * nv : (a + 1) * nv], in_=best[:])

@@ -33,27 +33,27 @@ def tile_picked_zlateq_relu_p_kernel(tc, x_words, x_scales, w1, v_words, v_scale
         xs_win = keep.tile([P, T], U8, align_bytes=64)
         vs_win = keep.tile([P, G], U8, align_bytes=64)
         xw_win = keep.tile([P, T], U32, align_bytes=64)
-        vw_win = keep.tile([P, G], U32, align_bytes=64)
-        zero = keep.tile([P, 8], F32)
-        warm_out = keep.tile([P, 8], F32)
+        zero = keep.tile([P, 8], F32, align_bytes=64, tag="after_cast")
+        warm_out = keep.tile([P, 8], F32, align_bytes=64, tag="after_warm")
 
         nc.vector.memset(vs_win[:].bitcast(I32), 0)
         nc.vector.memset(zero[:], 0.0)
-        nc.scalar.activation(warm_out[:], zero[:], RELU)
 
         nc.sync.dma_start(offs_sb[:], offs)
         for q in range(4):
             rows = x_scales[0, 4 * q : 4 * q + 4, :].bitcast(I32)
-            nc.sync.dma_start(out=xs_win[32 * q : 32 * q + 32, :].bitcast(I32), in_=rows.partition_broadcast(8))
-        nc.sync.dma_start(doc_sb[:], doc)
+            (nc.sync if q < 2 else nc.scalar).dma_start(out=xs_win[32 * q : 32 * q + 32, :].bitcast(I32), in_=rows.partition_broadcast(8))
         nc.sync.dma_start(out=xw_win[:].bitcast(I32), in_=x_words[0].rearrange("p n r -> p (n r)").bitcast(I32))
         w_rows = w1.rearrange("(p j) i -> p j i", j=PACK)
         w_first = keep.tile([P, PACK, W_SPLIT], F32)
-        w_last = keep.tile([P, PACK, H - W_SPLIT], F32, align_bytes=64, tag="after_cast")
         nc.sync.dma_start(out=w_first[:], in_=w_rows[:, :, :W_SPLIT])
+        nc.sync.dma_start(doc_sb[:], doc)
+        nc.scalar.activation(warm_out[:], zero[:], RELU)
         for q in range(4):
             nc.sync.dma_start(out=vs_win[32 * q : 32 * q + 4, :].bitcast(I32), in_=v_scales[0, 4 * q : 4 * q + 4, :].bitcast(I32))
+        w_last = keep.tile([P, PACK, H - W_SPLIT], F32, align_bytes=64, tag="after_cast")
         nc.sync.dma_start(out=w_last[:], in_=w_rows[:, :, W_SPLIT:])
+        vw_win = keep.tile([P, G], U32, align_bytes=64, tag="after_warm")
         nc.sync.dma_start(out=vw_win[:].bitcast(I32), in_=v_words[0].rearrange("p n r -> p (n r)").bitcast(I32))
 
         xs = keep.tile([P, S], U8, align_bytes=64)
@@ -72,8 +72,7 @@ def tile_picked_zlateq_relu_p_kernel(tc, x_words, x_scales, w1, v_words, v_scale
         nc.vector.quantize_mx(out=w_codes[:].bitcast(FP8X4), scales=w_scales[:], in_=w_bf[:])
 
         vw = keep.tile([P, V], U32, align_bytes=64, tag="after_cast")
-        nc.vector.tensor_copy(vw[:, :BANK], vw_win[:].indirect(doc_sb[:, : BANK // 16]))
-        nc.vector.tensor_copy(vw[:, BANK:], vw_win[:].indirect(doc_sb[:, BANK // 16 :]))
+        nc.vector.tensor_copy(vw[:], vw_win[:].indirect(doc_sb[:]))
 
         blocks = S // P
         h_codes = []
@@ -116,10 +115,7 @@ def tile_picked_zlateq_relu_p_kernel(tc, x_words, x_scales, w1, v_words, v_scale
                     stop=True,
                 )
                 best = keep.tile([P, nv], F32, name="best%d_%d" % (a, b))
-                if blocks * a + b in (0, 3, 6):
-                    nc.vector.tensor_reduce(best[:], y_acc[:].rearrange("p (v d) -> p v d", d=D), mybir.AxisListType.X, MAX)
-                else:
-                    y_sb = keep.tile([P, BANK], F32, name="y_sb%d_%d" % (a, b))
-                    nc.scalar.activation(y_sb[:], y_acc[:], COPY)
-                    nc.vector.tensor_tensor(best[:], y_sb[:, 0::2], y_sb[:, 1::2], MAX)
+                odd = keep.tile([P, nv], F32, name="odd%d_%d" % (a, b))
+                nc.scalar.activation(odd[:], y_acc[:, 1::2], COPY)
+                nc.vector.tensor_tensor(best[:], y_acc[:, 0::2], odd[:], MAX)
                 nc.sync.dma_start(out=out[b * P : (b + 1) * P, a * nv : (a + 1) * nv], in_=best[:])

@@ -20,6 +20,8 @@ P = 128
 PACK = 4
 BANK = 512
 W_SPLIT = 256
+V_SPLIT = 768
+V_EARLY = 512
 
 
 def tile_picked_zlateq_relu_p_kernel(tc, x_words, x_scales, w1, v_words, v_scales, offs, doc, out):
@@ -33,35 +35,31 @@ def tile_picked_zlateq_relu_p_kernel(tc, x_words, x_scales, w1, v_words, v_scale
         xs_win = keep.tile([P, T], U8, align_bytes=64)
         vs_win = keep.tile([P, G], U8, align_bytes=64)
         xw_win = keep.tile([P, T], U32, align_bytes=64)
-        zero = keep.tile([P, 8], F32, align_bytes=64, tag="after_cast")
-        warm_out = keep.tile([P, 8], F32, align_bytes=64, tag="after_warm")
-
-        nc.vector.memset(vs_win[:].bitcast(I32), 0)
-        nc.vector.memset(zero[:], 0.0)
-
-        nc.sync.dma_start(offs_sb[:], offs)
-        for q in range(4):
-            rows = x_scales[0, 4 * q : 4 * q + 4, :].bitcast(I32)
-            (nc.sync if q < 2 else nc.scalar).dma_start(out=xs_win[32 * q : 32 * q + 32, :].bitcast(I32), in_=rows.partition_broadcast(8))
-        nc.sync.dma_start(out=xw_win[:].bitcast(I32), in_=x_words[0].rearrange("p n r -> p (n r)").bitcast(I32))
-        w_rows = w1.rearrange("(p j) i -> p j i", j=PACK)
+        vw_win = keep.tile([P, G], U32, align_bytes=64)
         w_first = keep.tile([P, PACK, W_SPLIT], F32)
-        nc.sync.dma_start(out=w_first[:], in_=w_rows[:, :, :W_SPLIT])
+        w_last = keep.tile([P, PACK, H - W_SPLIT], F32)
+
+        nc.vector.memset(xs_win[:].bitcast(I32), 0)
+
+        w_rows = w1.rearrange("(p j) i -> p j i", j=PACK)
         nc.sync.dma_start(doc_sb[:], doc)
-        nc.scalar.activation(warm_out[:], zero[:], RELU)
         for q in range(4):
-            nc.sync.dma_start(out=vs_win[32 * q : 32 * q + 4, :].bitcast(I32), in_=v_scales[0, 4 * q : 4 * q + 4, :].bitcast(I32))
-        w_last = keep.tile([P, PACK, H - W_SPLIT], F32, align_bytes=64, tag="after_cast")
+            rows = v_scales[0, 4 * q : 4 * q + 4, :].bitcast(I32)
+            (nc.sync if q < 2 else nc.scalar).dma_start(out=vs_win[32 * q : 32 * q + 32, :].bitcast(I32), in_=rows.partition_broadcast(8))
+        nc.sync.dma_start(offs_sb[:], offs)
+        nc.sync.dma_start(out=w_first[:], in_=w_rows[:, :, :W_SPLIT])
         nc.sync.dma_start(out=w_last[:], in_=w_rows[:, :, W_SPLIT:])
-        vw_win = keep.tile([P, G], U32, align_bytes=64, tag="after_warm")
-        nc.sync.dma_start(out=vw_win[:].bitcast(I32), in_=v_words[0].rearrange("p n r -> p (n r)").bitcast(I32))
+        for q in range(4):
+            nc.sync.dma_start(out=xs_win[32 * q : 32 * q + 4, :].bitcast(I32), in_=x_scales[0, 4 * q : 4 * q + 4, :].bitcast(I32))
+        v_rows = v_words[0].rearrange("p n r -> p (n r)").bitcast(I32)
+        nc.sync.dma_start(out=vw_win[:].bitcast(I32)[:, :V_EARLY], in_=v_rows[:, :V_EARLY])
+        nc.sync.dma_start(out=xw_win[:].bitcast(I32), in_=x_words[0].rearrange("p n r -> p (n r)").bitcast(I32))
+        nc.sync.dma_start(out=vw_win[:].bitcast(I32)[:, V_EARLY:], in_=v_rows[:, V_EARLY:])
 
         xs = keep.tile([P, S], U8, align_bytes=64)
-        xw = keep.tile([P, S], U32, align_bytes=64)
         vs = keep.tile([P, V], U8, align_bytes=64)
-        nc.vector.tensor_copy(xs[:], xs_win[:].indirect(offs_sb[:]))
-        nc.vector.tensor_copy(xw[:], xw_win[:].indirect(offs_sb[:]))
         nc.vector.tensor_copy(vs[:], vs_win[:].indirect(doc_sb[:]))
+        nc.vector.tensor_copy(xs[:], xs_win[:].indirect(offs_sb[:]))
 
         w_bf = keep.tile([P, H * PACK], BF16, align_bytes=64)
         w_dst = w_bf[:].rearrange("p (t m j) -> p m j t", t=PACK, j=PACK)
@@ -71,13 +69,16 @@ def tile_picked_zlateq_relu_p_kernel(tc, x_words, x_scales, w1, v_words, v_scale
         w_scales = keep.tile([P, H], U8, align_bytes=64)
         nc.vector.quantize_mx(out=w_codes[:].bitcast(FP8X4), scales=w_scales[:], in_=w_bf[:])
 
-        vw = keep.tile([P, V], U32, align_bytes=64, tag="after_cast")
-        nc.vector.tensor_copy(vw[:], vw_win[:].indirect(doc_sb[:]))
-
         blocks = S // P
-        h_codes = []
-        h_scales = []
-        for b in range(blocks):
+        xw = []
+        for first, last in ((0, 1), (1, 2), (2, 4)):
+            piece = keep.tile([P, (last - first) * P], U32, align_bytes=64, name="xw%d" % first)
+            nc.vector.tensor_copy(piece[:], xw_win[:].indirect(offs_sb[:, first * 8 : last * 8]))
+            xw.extend(piece[:, i * P : (i + 1) * P] for i in range(last - first))
+
+        h_bf, h_codes, h_scales, vw = [], [], [], []
+
+        def project(b):
             h_acc = psum.tile([P, BANK], F32, tag="bank", name="h_acc%d" % b)
             cols = slice(b * P, (b + 1) * P)
             for t in range(PACK):
@@ -86,36 +87,59 @@ def tile_picked_zlateq_relu_p_kernel(tc, x_words, x_scales, w1, v_words, v_scale
                     out=h_acc[:, ch],
                     lhsT=w_codes[:, ch].bitcast(FP8X4),
                     lhsT_scale=w_scales[:, ch],
-                    rhs=xw[:, cols].bitcast(FP8X4),
+                    rhs=xw[b].bitcast(FP8X4),
                     rhs_scale=xs[:, cols],
                     start=True,
                     stop=True,
                 )
-            h_bf = keep.tile([P, P * PACK], BF16, align_bytes=64, name="h_bf%d" % b)
+            if b % 2 == 0:
+                h_bf.append(keep.tile([P, 2 * P * PACK], BF16, align_bytes=64, name="h_bf%d" % b, tag="h_bf%d" % b))
             nc.scalar.activation(
-                h_bf[:].rearrange("p (n t) -> p n t", t=PACK),
+                h_bf[b // 2][:, (b % 2) * BANK : (b % 2 + 1) * BANK].rearrange("p (n t) -> p n t", t=PACK),
                 h_acc[:].rearrange("p (t n) -> p n t", t=PACK),
                 RELU,
             )
-            h_codes.append(keep.tile([P, P], U32, align_bytes=64, name="h_codes%d" % b))
-            h_scales.append(keep.tile([P, P], U8, align_bytes=64, name="h_scales%d" % b))
-            nc.vector.quantize_mx(out=h_codes[b][:].bitcast(FP8X4), scales=h_scales[b][:], in_=h_bf[:])
+
+        def quantise(pair):
+            codes = keep.tile([P, 2 * P], U32, align_bytes=64, name="h_codes%d" % pair)
+            scales = keep.tile([P, 2 * P], U8, align_bytes=64, name="h_scales%d" % pair)
+            nc.vector.quantize_mx(out=codes[:].bitcast(FP8X4), scales=scales[:], in_=h_bf[pair][:])
+            h_codes.extend(codes[:, i * P : (i + 1) * P] for i in range(2))
+            h_scales.extend(scales[:, i * P : (i + 1) * P] for i in range(2))
+
+        def gather_docs(first, last, tag):
+            vw.append(keep.tile([P, last - first], U32, align_bytes=64, name="vw%d" % first, tag=tag))
+            nc.vector.tensor_copy(vw[-1][:], vw_win[:].indirect(doc_sb[:, first // 16 : last // 16]))
 
         nv = BANK // D
-        for a in range(V // BANK):
-            for b in range(blocks):
-                y_acc = psum.tile([P, BANK], F32, tag="bank", name="y_acc%d_%d" % (a, b))
+
+        def score(a, b):
+            y_acc = psum.tile([P, BANK], F32, tag="bank", name="y_acc%d_%d" % (a, b))
+            cuts = [a * BANK, (a + 1) * BANK] if (a + 1) * BANK <= V_SPLIT else [a * BANK, V_SPLIT, (a + 1) * BANK]
+            for first, last in zip(cuts, cuts[1:]):
+                words = vw[0][:, first:last] if last <= V_SPLIT else vw[1][:, first - V_SPLIT : last - V_SPLIT]
                 nc.tensor.matmul_mx(
-                    out=y_acc[:],
-                    lhsT=h_codes[b][:].bitcast(FP8X4),
-                    lhsT_scale=h_scales[b][:],
-                    rhs=vw[:, a * BANK : (a + 1) * BANK].bitcast(FP8X4),
-                    rhs_scale=vs[:, a * BANK : (a + 1) * BANK],
+                    out=y_acc[:, first - a * BANK : last - a * BANK],
+                    lhsT=h_codes[b].bitcast(FP8X4),
+                    lhsT_scale=h_scales[b],
+                    rhs=words.bitcast(FP8X4),
+                    rhs_scale=vs[:, first:last],
                     start=True,
                     stop=True,
                 )
-                best = keep.tile([P, nv], F32, name="best%d_%d" % (a, b))
-                odd = keep.tile([P, nv], F32, name="odd%d_%d" % (a, b))
-                nc.scalar.activation(odd[:], y_acc[:, 1::2], COPY)
-                nc.vector.tensor_tensor(best[:], y_acc[:, 0::2], odd[:], MAX)
-                nc.sync.dma_start(out=out[b * P : (b + 1) * P, a * nv : (a + 1) * nv], in_=best[:])
+            best = keep.tile([P, nv], F32, name="best%d_%d" % (a, b))
+            odd = keep.tile([P, nv], F32, name="odd%d_%d" % (a, b))
+            nc.scalar.activation(odd[:], y_acc[:, 1::2], COPY)
+            nc.vector.tensor_tensor(best[:], y_acc[:, 0::2], odd[:], MAX)
+            nc.sync.dma_start(out=out[b * P : (b + 1) * P, a * nv : (a + 1) * nv], in_=best[:])
+
+        for b in range(blocks):
+            project(b)
+        gather_docs(0, V_SPLIT, "vw0")
+        quantise(0)
+        gather_docs(V_SPLIT, V, "h_bf0")
+        quantise(1)
+        for pair in range(2):
+            for a in range(2):
+                for b in (2 * pair, 2 * pair + 1):
+                    score(a, b)

@@ -39,13 +39,16 @@ def tile_picked_zlateq_relu_p_kernel(tc, x_words, x_scales, w1, v_words, v_scale
         w_first = keep.tile([P, PACK, W_SPLIT], F32)
         w_last = keep.tile([P, PACK, H - W_SPLIT], F32)
 
+        vs = keep.tile([P, V], U8, align_bytes=64)
         nc.vector.memset(xs_win[:].bitcast(I32), 0)
+        nc.vector.memset(vs_win[32:64, :].bitcast(I32), 0)
+        nc.vector.memset(vs_win[64:, :].bitcast(I32), 0)
+        nc.vector.memset(vs[:].bitcast(I32), 0)
 
         w_rows = w1.rearrange("(p j) i -> p j i", j=PACK)
         nc.sync.dma_start(doc_sb[:], doc)
-        for q in range(4):
-            rows = v_scales[0, 4 * q : 4 * q + 4, :].bitcast(I32)
-            (nc.sync if q < 2 else nc.scalar).dma_start(out=vs_win[32 * q : 32 * q + 32, :].bitcast(I32), in_=rows.partition_broadcast(8))
+        v_twice = v_scales[0].bitcast(I32).unsqueeze(1).broadcast_to([16, 2, G // 4])
+        nc.sync.dma_start(out=vs_win[:32, :].bitcast(I32), in_=v_twice)
         nc.sync.dma_start(offs_sb[:], offs)
         nc.sync.dma_start(out=w_first[:], in_=w_rows[:, :, :W_SPLIT])
         nc.sync.dma_start(out=w_last[:], in_=w_rows[:, :, W_SPLIT:])
@@ -57,8 +60,10 @@ def tile_picked_zlateq_relu_p_kernel(tc, x_words, x_scales, w1, v_words, v_scale
         nc.sync.dma_start(out=vw_win[:].bitcast(I32)[:, V_EARLY:], in_=v_rows[:, V_EARLY:])
 
         xs = keep.tile([P, S], U8, align_bytes=64)
-        vs = keep.tile([P, V], U8, align_bytes=64)
-        nc.vector.tensor_copy(vs[:], vs_win[:].indirect(doc_sb[:]))
+        vs_rows = keep.tile([P, V], U8, align_bytes=64)
+        nc.vector.tensor_copy(vs_rows[:], vs_win[:].indirect(doc_sb[:]))
+        for q in range(4):
+            nc.sync.dma_start(out=vs[32 * q : 32 * q + 4, :].bitcast(I32), in_=vs_rows[8 * q : 8 * q + 8 : 2, :].bitcast(I32))
         nc.vector.tensor_copy(xs[:], xs_win[:].indirect(offs_sb[:]))
 
         w_bf = keep.tile([P, H * PACK], BF16, align_bytes=64)

@@ -77,7 +77,7 @@ def tile_picked_zlateq_relu_p_kernel(tc, x_words, x_scales, w1, v_words, v_scale
         blocks = S // P
         xw = []
         for first, last in ((0, 1), (1, 2), (2, 4)):
-            piece = keep.tile([P, (last - first) * P], U32, align_bytes=64, name="xw%d" % first)
+            piece = keep.tile([P, (last - first) * P], U32, align_bytes=64, name="xw%d" % first, tag="xw%d" % first)
             nc.vector.tensor_copy(piece[:], xw_win[:].indirect(offs_sb[:, first * 8 : last * 8]))
             xw.extend(piece[:, i * P : (i + 1) * P] for i in range(last - first))
 
@@ -142,7 +142,7 @@ def tile_picked_zlateq_relu_p_kernel(tc, x_words, x_scales, w1, v_words, v_scale
             project(b)
         gather_docs(0, V_SPLIT, "vw0")
         quantise(0)
-        gather_docs(V_SPLIT, V, "h_bf0")
+        gather_docs(V_SPLIT, V, "xw2")
         quantise(1)
         for pair in range(2):
             for a in range(2):

@@ -19,15 +19,14 @@ MAX = mybir.AluOpType.max
 P = 128
 PACK = 4
 BANK = 512
-W_SPLIT = 256
 V_SPLIT = 768
-V_EARLY = 512
 
 
 def tile_picked_zlateq_relu_p_kernel(tc, x_words, x_scales, w1, v_words, v_scales, offs, doc, out):
     nc = tc.nc
     with ExitStack() as ctx:
         keep = ctx.enter_context(tc.tile_pool(name="keep", bufs=1))
+        late = ctx.enter_context(tc.tile_pool(name="late", bufs=1))
         psum = ctx.enter_context(tc.psum_pool(name="psum", bufs=8))
 
         offs_sb = keep.tile([P, S // 16], U16)
@@ -36,8 +35,7 @@ def tile_picked_zlateq_relu_p_kernel(tc, x_words, x_scales, w1, v_words, v_scale
         vs_win = keep.tile([P, G], U8, align_bytes=64)
         xw_win = keep.tile([P, T], U32, align_bytes=64)
         vw_win = keep.tile([P, G], U32, align_bytes=64)
-        w_first = keep.tile([P, PACK, W_SPLIT], F32)
-        w_last = keep.tile([P, PACK, H - W_SPLIT], F32)
+        w_raw = keep.tile([P, PACK * H], F32, align_bytes=64, tag="w_raw")
 
         vs = keep.tile([P, V], U8, align_bytes=64)
         nc.vector.memset(xs_win[:].bitcast(I32), 0)
@@ -45,41 +43,45 @@ def tile_picked_zlateq_relu_p_kernel(tc, x_words, x_scales, w1, v_words, v_scale
         nc.vector.memset(vs_win[64:, :].bitcast(I32), 0)
         nc.vector.memset(vs[:].bitcast(I32), 0)
 
-        w_rows = w1.rearrange("(p j) i -> p j i", j=PACK)
         nc.sync.dma_start(doc_sb[:], doc)
         v_twice = v_scales[0].bitcast(I32).unsqueeze(1).broadcast_to([16, 2, G // 4])
         nc.sync.dma_start(out=vs_win[:32, :].bitcast(I32), in_=v_twice)
         nc.sync.dma_start(offs_sb[:], offs)
-        nc.sync.dma_start(out=w_first[:], in_=w_rows[:, :, :W_SPLIT])
-        nc.sync.dma_start(out=w_last[:], in_=w_rows[:, :, W_SPLIT:])
+        nc.sync.dma_start(out=w_raw[:], in_=w1.rearrange("(p j) i -> p (j i)", j=PACK))
         for q in range(4):
             nc.sync.dma_start(out=xs_win[32 * q : 32 * q + 4, :].bitcast(I32), in_=x_scales[0, 4 * q : 4 * q + 4, :].bitcast(I32))
-        v_rows = v_words[0].rearrange("p n r -> p (n r)").bitcast(I32)
-        nc.sync.dma_start(out=vw_win[:].bitcast(I32)[:, :V_EARLY], in_=v_rows[:, :V_EARLY])
         nc.sync.dma_start(out=xw_win[:].bitcast(I32), in_=x_words[0].rearrange("p n r -> p (n r)").bitcast(I32))
-        nc.sync.dma_start(out=vw_win[:].bitcast(I32)[:, V_EARLY:], in_=v_rows[:, V_EARLY:])
+        nc.sync.dma_start(out=vw_win[:].bitcast(I32), in_=v_words[0].rearrange("p n r -> p (n r)").bitcast(I32))
 
         xs = keep.tile([P, S], U8, align_bytes=64)
-        vs_rows = keep.tile([P, V], U8, align_bytes=64)
+        vs_rows = late.tile([P, V], U8, align_bytes=64, offset=0)
         nc.vector.tensor_copy(vs_rows[:], vs_win[:].indirect(doc_sb[:]))
         for q in range(4):
             nc.sync.dma_start(out=vs[32 * q : 32 * q + 4, :].bitcast(I32), in_=vs_rows[8 * q : 8 * q + 8 : 2, :].bitcast(I32))
         nc.vector.tensor_copy(xs[:], xs_win[:].indirect(offs_sb[:]))
 
-        w_bf = keep.tile([P, H * PACK], BF16, align_bytes=64)
-        w_dst = w_bf[:].rearrange("p (t m j) -> p m j t", t=PACK, j=PACK)
-        nc.scalar.activation(w_dst[:, : W_SPLIT // PACK], w_first[:].rearrange("p j (m t) -> p m j t", t=PACK), COPY)
-        nc.scalar.activation(w_dst[:, W_SPLIT // PACK :], w_last[:].rearrange("p j (m t) -> p m j t", t=PACK), COPY)
-        w_codes = keep.tile([P, H], U32, align_bytes=64)
-        w_scales = keep.tile([P, H], U8, align_bytes=64)
-        nc.vector.quantize_mx(out=w_codes[:].bitcast(FP8X4), scales=w_scales[:], in_=w_bf[:])
+        w_codes, w_scales, xw = [], [], []
+        w_src = w_raw[:].rearrange("p (j m u t) -> p u m j t", j=PACK, u=2, t=2)
+
+        def quantise_w(u):
+            w_bf = keep.tile([P, 2 * P * PACK], BF16, align_bytes=64, name="w_bf%d" % u)
+            nc.scalar.activation(w_bf[:].rearrange("p (t m j) -> p m j t", t=2, j=PACK), w_src[:, u], COPY)
+            codes = keep.tile([P, 2 * P], U32, align_bytes=64, name="w_codes%d" % u)
+            scales = keep.tile([P, 2 * P], U8, align_bytes=64, name="w_scales%d" % u)
+            nc.vector.quantize_mx(out=codes[:].bitcast(FP8X4), scales=scales[:], in_=w_bf[:])
+            w_codes.extend(codes[:, i * P : (i + 1) * P] for i in range(2))
+            w_scales.extend(scales[:, i * P : (i + 1) * P] for i in range(2))
+
+        def gather_tokens(pair, tag):
+            piece = keep.tile([P, 2 * P], U32, align_bytes=64, name="xw%d" % pair, tag=tag)
+            nc.vector.tensor_copy(piece[:], xw_win[:].indirect(offs_sb[:, pair * 16 : (pair + 1) * 16]))
+            xw.extend(piece[:, i * P : (i + 1) * P] for i in range(2))
 
         blocks = S // P
-        xw = []
-        for first, last in ((0, 1), (1, 2), (2, 4)):
-            piece = keep.tile([P, (last - first) * P], U32, align_bytes=64, name="xw%d" % first, tag="xw%d" % first)
-            nc.vector.tensor_copy(piece[:], xw_win[:].indirect(offs_sb[:, first * 8 : last * 8]))
-            xw.extend(piece[:, i * P : (i + 1) * P] for i in range(last - first))
+        quantise_w(0)
+        gather_tokens(0, "xw0")
+        quantise_w(1)
+        gather_tokens(1, "w_raw")
 
         h_bf, h_codes, h_scales, vw = [], [], [], []
 
@@ -90,8 +92,8 @@ def tile_picked_zlateq_relu_p_kernel(tc, x_words, x_scales, w1, v_words, v_scale
                 ch = slice(t * P, (t + 1) * P)
                 nc.tensor.matmul_mx(
                     out=h_acc[:, ch],
-                    lhsT=w_codes[:, ch].bitcast(FP8X4),
-                    lhsT_scale=w_scales[:, ch],
+                    lhsT=w_codes[t].bitcast(FP8X4),
+                    lhsT_scale=w_scales[t],
                     rhs=xw[b].bitcast(FP8X4),
                     rhs_scale=xs[:, cols],
                     start=True,
@@ -107,14 +109,14 @@ def tile_picked_zlateq_relu_p_kernel(tc, x_words, x_scales, w1, v_words, v_scale
 
         def quantise(pair):
             codes = keep.tile([P, 2 * P], U32, align_bytes=64, name="h_codes%d" % pair)
-            scales = keep.tile([P, 2 * P], U8, align_bytes=64, name="h_scales%d" % pair)
+            scales = late.tile([P, 2 * P], U8, align_bytes=64, name="h_scales%d" % pair, offset=2 * P * pair)
             nc.vector.quantize_mx(out=codes[:].bitcast(FP8X4), scales=scales[:], in_=h_bf[pair][:])
             h_codes.extend(codes[:, i * P : (i + 1) * P] for i in range(2))
             h_scales.extend(scales[:, i * P : (i + 1) * P] for i in range(2))
 
-        def gather_docs(first, last, tag):
-            vw.append(keep.tile([P, last - first], U32, align_bytes=64, name="vw%d" % first, tag=tag))
-            nc.vector.tensor_copy(vw[-1][:], vw_win[:].indirect(doc_sb[:, first // 16 : last // 16]))
+        def gather_docs(first, last, words):
+            vw.append(words)
+            nc.vector.tensor_copy(words[:], vw_win[:].indirect(doc_sb[:, first // 16 : last // 16]))
 
         nv = BANK // D
 
@@ -140,9 +142,9 @@ def tile_picked_zlateq_relu_p_kernel(tc, x_words, x_scales, w1, v_words, v_scale
 
         for b in range(blocks):
             project(b)
-        gather_docs(0, V_SPLIT, "vw0")
+        gather_docs(0, V_SPLIT, keep.tile([P, V_SPLIT], U32, align_bytes=64, name="vw_first"))
         quantise(0)
-        gather_docs(V_SPLIT, V, "xw2")
+        gather_docs(V_SPLIT, V, late.tile([P, V - V_SPLIT], U32, align_bytes=64, name="vw_last", offset=4 * P))
         quantise(1)
         for pair in range(2):
             for a in range(2):

@@ -19,7 +19,6 @@ MAX = mybir.AluOpType.max
 P = 128
 PACK = 4
 BANK = 512
-V_SPLIT = 768
 
 
 def tile_picked_zlateq_relu_p_kernel(tc, x_words, x_scales, w1, v_words, v_scales, offs, doc, out):
@@ -39,25 +38,24 @@ def tile_picked_zlateq_relu_p_kernel(tc, x_words, x_scales, w1, v_words, v_scale
 
         vs = keep.tile([P, V], U8, align_bytes=64)
         nc.vector.memset(xs_win[:].bitcast(I32), 0)
-        nc.vector.memset(vs_win[32:64, :].bitcast(I32), 0)
-        nc.vector.memset(vs_win[64:, :].bitcast(I32), 0)
+        nc.vector.memset(vs_win[:96, :].bitcast(I32), 0)
+        nc.vector.memset(vs_win[96:112, :].bitcast(I32), 0)
         nc.vector.memset(vs[:].bitcast(I32), 0)
 
+        nc.sync.dma_start(out=vs_win[112:, :].bitcast(I32), in_=v_scales[0].bitcast(I32))
         nc.sync.dma_start(doc_sb[:], doc)
-        v_twice = v_scales[0].bitcast(I32).unsqueeze(1).broadcast_to([16, 2, G // 4])
-        nc.sync.dma_start(out=vs_win[:32, :].bitcast(I32), in_=v_twice)
         nc.sync.dma_start(offs_sb[:], offs)
         nc.sync.dma_start(out=w_raw[:], in_=w1.rearrange("(p j) i -> p (j i)", j=PACK))
-        for q in range(4):
-            nc.sync.dma_start(out=xs_win[32 * q : 32 * q + 4, :].bitcast(I32), in_=x_scales[0, 4 * q : 4 * q + 4, :].bitcast(I32))
+        for r in range(4):
+            nc.sync.dma_start(out=xs_win[r:P:32, :].bitcast(I32), in_=x_scales[0, r:16:4, :].bitcast(I32))
         nc.sync.dma_start(out=xw_win[:].bitcast(I32), in_=x_words[0].rearrange("p n r -> p (n r)").bitcast(I32))
         nc.sync.dma_start(out=vw_win[:].bitcast(I32), in_=v_words[0].rearrange("p n r -> p (n r)").bitcast(I32))
 
         xs = keep.tile([P, S], U8, align_bytes=64)
-        vs_rows = late.tile([P, V], U8, align_bytes=64, offset=0)
+        vs_rows = late.tile([P, V], U8, align_bytes=64, offset=1024)
         nc.vector.tensor_copy(vs_rows[:], vs_win[:].indirect(doc_sb[:]))
-        for q in range(4):
-            nc.sync.dma_start(out=vs[32 * q : 32 * q + 4, :].bitcast(I32), in_=vs_rows[8 * q : 8 * q + 8 : 2, :].bitcast(I32))
+        for r in range(4):
+            nc.sync.dma_start(out=vs[r:P:32, :].bitcast(I32), in_=vs_rows[112 + r : P : 4, :].bitcast(I32))
         nc.vector.tensor_copy(xs[:], xs_win[:].indirect(offs_sb[:]))
 
         w_codes, w_scales, xw = [], [], []
@@ -83,7 +81,8 @@ def tile_picked_zlateq_relu_p_kernel(tc, x_words, x_scales, w1, v_words, v_scale
         quantise_w(1)
         gather_tokens(1, "w_raw")
 
-        h_bf, h_codes, h_scales, vw = [], [], [], []
+        h_bf = keep.tile([P, blocks * BANK], BF16, align_bytes=64)
+        h_codes, h_scales, vw = [], [], []
 
         def project(b):
             h_acc = psum.tile([P, BANK], F32, tag="bank", name="h_acc%d" % b)
@@ -99,41 +98,39 @@ def tile_picked_zlateq_relu_p_kernel(tc, x_words, x_scales, w1, v_words, v_scale
                     start=True,
                     stop=True,
                 )
-            if b % 2 == 0:
-                h_bf.append(keep.tile([P, 2 * P * PACK], BF16, align_bytes=64, name="h_bf%d" % b, tag="h_bf%d" % b))
             nc.scalar.activation(
-                h_bf[b // 2][:, (b % 2) * BANK : (b % 2 + 1) * BANK].rearrange("p (n t) -> p n t", t=PACK),
+                h_bf[:, b * BANK : (b + 1) * BANK].rearrange("p (n t) -> p n t", t=PACK),
                 h_acc[:].rearrange("p (t n) -> p n t", t=PACK),
                 RELU,
             )
 
-        def quantise(pair):
-            codes = keep.tile([P, 2 * P], U32, align_bytes=64, name="h_codes%d" % pair)
-            scales = late.tile([P, 2 * P], U8, align_bytes=64, name="h_scales%d" % pair, offset=2 * P * pair)
-            nc.vector.quantize_mx(out=codes[:].bitcast(FP8X4), scales=scales[:], in_=h_bf[pair][:])
-            h_codes.extend(codes[:, i * P : (i + 1) * P] for i in range(2))
-            h_scales.extend(scales[:, i * P : (i + 1) * P] for i in range(2))
+        def quantise(first, last):
+            width = (last - first) * P
+            codes = keep.tile([P, width], U32, align_bytes=64, name="h_codes%d" % first)
+            scales = late.tile([P, width], U8, align_bytes=64, name="h_scales%d" % first, offset=1088 + first * P)
+            nc.vector.quantize_mx(out=codes[:].bitcast(FP8X4), scales=scales[:], in_=h_bf[:, first * BANK : last * BANK])
+            h_codes.extend(codes[:, i * P : (i + 1) * P] for i in range(last - first))
+            h_scales.extend(scales[:, i * P : (i + 1) * P] for i in range(last - first))
 
         def gather_docs(first, last, words):
-            vw.append(words)
+            vw.append((first, last, words))
             nc.vector.tensor_copy(words[:], vw_win[:].indirect(doc_sb[:, first // 16 : last // 16]))
 
         nv = BANK // D
 
         def score(a, b):
             y_acc = psum.tile([P, BANK], F32, tag="bank", name="y_acc%d_%d" % (a, b))
-            cuts = [a * BANK, (a + 1) * BANK] if (a + 1) * BANK <= V_SPLIT else [a * BANK, V_SPLIT, (a + 1) * BANK]
-            for first, last in zip(cuts, cuts[1:]):
-                words = vw[0][:, first:last] if last <= V_SPLIT else vw[1][:, first - V_SPLIT : last - V_SPLIT]
-                nc.tensor.matmul_mx(
-                    out=y_acc[:, first - a * BANK : last - a * BANK],
-                    lhsT=h_codes[b].bitcast(FP8X4),
-                    lhsT_scale=h_scales[b],
-                    rhs=words.bitcast(FP8X4),
-                    rhs_scale=vs[:, first:last],
-                    start=True,
-                    stop=True,
-                )
+            for first, last, words in vw:
+                if first // BANK == a:
+                    nc.tensor.matmul_mx(
+                        out=y_acc[:, first - a * BANK : last - a * BANK],
+                        lhsT=h_codes[b].bitcast(FP8X4),
+                        lhsT_scale=h_scales[b],
+                        rhs=words[:].bitcast(FP8X4),
+                        rhs_scale=vs[:, first:last],
+                        start=True,
+                        stop=True,
+                    )
             best = keep.tile([P, nv], F32, name="best%d_%d" % (a, b))
             odd = keep.tile([P, nv], F32, name="odd%d_%d" % (a, b))
             nc.scalar.activation(odd[:], y_acc[:, 1::2], COPY)
@@ -142,10 +139,12 @@ def tile_picked_zlateq_relu_p_kernel(tc, x_words, x_scales, w1, v_words, v_scale
 
         for b in range(blocks):
             project(b)
-        gather_docs(0, V_SPLIT, keep.tile([P, V_SPLIT], U32, align_bytes=64, name="vw_first"))
-        quantise(0)
-        gather_docs(V_SPLIT, V, late.tile([P, V - V_SPLIT], U32, align_bytes=64, name="vw_last", offset=4 * P))
-        quantise(1)
+        gather_docs(0, 512, keep.tile([P, 512], U32, align_bytes=64, name="vw0"))
+        quantise(0, 1)
+        gather_docs(512, 768, late.tile([P, 256], U32, align_bytes=64, name="vw1", offset=64))
+        quantise(1, 2)
+        gather_docs(768, 1024, late.tile([P, 256], U32, align_bytes=64, name="vw2", offset=1600))
+        quantise(2, 4)
         for pair in range(2):
             for a in range(2):
                 for b in (2 * pair, 2 * pair + 1):

@@ -52,7 +52,7 @@ def tile_picked_zlateq_relu_p_kernel(tc, x_words, x_scales, w1, v_words, v_scale
         nc.sync.dma_start(out=vw_win[:].bitcast(I32), in_=v_words[0].rearrange("p n r -> p (n r)").bitcast(I32))
 
         xs = keep.tile([P, S], U8, align_bytes=64)
-        vs_rows = late.tile([P, V], U8, align_bytes=64, offset=1024)
+        vs_rows = late.tile([P, V], U8, align_bytes=64, offset=1984)
         nc.vector.tensor_copy(vs_rows[:], vs_win[:].indirect(doc_sb[:]))
         for r in range(4):
             nc.sync.dma_start(out=vs[r:P:32, :].bitcast(I32), in_=vs_rows[112 + r : P : 4, :].bitcast(I32))
@@ -82,7 +82,7 @@ def tile_picked_zlateq_relu_p_kernel(tc, x_words, x_scales, w1, v_words, v_scale
         gather_tokens(1, "w_raw")
 
         h_bf = keep.tile([P, blocks * BANK], BF16, align_bytes=64)
-        h_codes, h_scales, vw = [], [], []
+        h_codes, h_scales = [], []
 
         def project(b):
             h_acc = psum.tile([P, BANK], F32, tag="bank", name="h_acc%d" % b)
@@ -104,48 +104,62 @@ def tile_picked_zlateq_relu_p_kernel(tc, x_words, x_scales, w1, v_words, v_scale
                 RELU,
             )
 
-        def quantise(first, last):
-            width = (last - first) * P
-            codes = keep.tile([P, width], U32, align_bytes=64, name="h_codes%d" % first)
-            scales = late.tile([P, width], U8, align_bytes=64, name="h_scales%d" % first, offset=1088 + first * P)
-            nc.vector.quantize_mx(out=codes[:].bitcast(FP8X4), scales=scales[:], in_=h_bf[:, first * BANK : last * BANK])
-            h_codes.extend(codes[:, i * P : (i + 1) * P] for i in range(last - first))
-            h_scales.extend(scales[:, i * P : (i + 1) * P] for i in range(last - first))
+        def quantise_h(b):
+            codes = keep.tile([P, P], U32, align_bytes=64, name="h_codes%d" % b)
+            scales = late.tile([P, P], U8, align_bytes=64, name="h_scales%d" % b, offset=2048 + b * P)
+            nc.vector.quantize_mx(out=codes[:].bitcast(FP8X4), scales=scales[:], in_=h_bf[:, b * BANK : (b + 1) * BANK])
+            h_codes.append(codes)
+            h_scales.append(scales)
 
-        def gather_docs(first, last, words):
-            vw.append((first, last, words))
-            nc.vector.tensor_copy(words[:], vw_win[:].indirect(doc_sb[:, first // 16 : last // 16]))
+        vw = [keep.tile([P, BANK], U32, align_bytes=64, name="vw0"), late.tile([P, BANK], U32, align_bytes=64, name="vw1", offset=0)]
+
+        def gather_docs(first, last):
+            a = first // BANK
+            nc.vector.tensor_copy(vw[a][:, first - a * BANK : last - a * BANK], vw_win[:].indirect(doc_sb[:, first // 16 : last // 16]))
 
         nv = BANK // D
+        y_acc = {}
 
-        def score(a, b):
-            y_acc = psum.tile([P, BANK], F32, tag="bank", name="y_acc%d_%d" % (a, b))
-            for first, last, words in vw:
-                if first // BANK == a:
-                    nc.tensor.matmul_mx(
-                        out=y_acc[:, first - a * BANK : last - a * BANK],
-                        lhsT=h_codes[b].bitcast(FP8X4),
-                        lhsT_scale=h_scales[b],
-                        rhs=words[:].bitcast(FP8X4),
-                        rhs_scale=vs[:, first:last],
-                        start=True,
-                        stop=True,
-                    )
+        def score(b, first, last):
+            a = first // BANK
+            if (a, b) not in y_acc:
+                y_acc[a, b] = psum.tile([P, BANK], F32, tag="bank", name="y_acc%d_%d" % (a, b))
+            cols = slice(first - a * BANK, last - a * BANK)
+            nc.tensor.matmul_mx(
+                out=y_acc[a, b][:, cols],
+                lhsT=h_codes[b][:].bitcast(FP8X4),
+                lhsT_scale=h_scales[b][:],
+                rhs=vw[a][:, cols].bitcast(FP8X4),
+                rhs_scale=vs[:, first:last],
+                start=True,
+                stop=True,
+            )
+
+        def finish(a, b):
             best = keep.tile([P, nv], F32, name="best%d_%d" % (a, b))
             odd = keep.tile([P, nv], F32, name="odd%d_%d" % (a, b))
-            nc.scalar.activation(odd[:], y_acc[:, 1::2], COPY)
-            nc.vector.tensor_tensor(best[:], y_acc[:, 0::2], odd[:], MAX)
+            nc.scalar.activation(odd[:], y_acc[a, b][:, 1::2], COPY)
+            nc.vector.tensor_tensor(best[:], y_acc[a, b][:, 0::2], odd[:], MAX)
             nc.sync.dma_start(out=out[b * P : (b + 1) * P, a * nv : (a + 1) * nv], in_=best[:])
 
         for b in range(blocks):
             project(b)
-        gather_docs(0, 512, keep.tile([P, 512], U32, align_bytes=64, name="vw0"))
-        quantise(0, 1)
-        gather_docs(512, 768, late.tile([P, 256], U32, align_bytes=64, name="vw1", offset=64))
-        quantise(1, 2)
-        gather_docs(768, 1024, late.tile([P, 256], U32, align_bytes=64, name="vw2", offset=1600))
-        quantise(2, 4)
-        for pair in range(2):
-            for a in range(2):
-                for b in (2 * pair, 2 * pair + 1):
-                    score(a, b)
+        gather_docs(0, 512)
+        quantise_h(0)
+        score(0, 0, 512)
+        gather_docs(512, 768)
+        quantise_h(1)
+        score(1, 0, 512)
+        score(0, 512, 768)
+        score(1, 512, 768)
+        quantise_h(2)
+        score(2, 0, 512)
+        score(2, 512, 768)
+        gather_docs(768, 1024)
+        for b in range(3):
+            score(b, 768, 1024)
+        quantise_h(3)
+        score(3, 0, 512)
+        score(3, 512, 1024)
+        for a, b in ((0, 0), (0, 1), (0, 2), (1, 0), (1, 1), (1, 2), (0, 3), (1, 3)):
+            finish(a, b)

@@ -70,16 +70,17 @@ def tile_picked_zlateq_relu_p_kernel(tc, x_words, x_scales, w1, v_words, v_scale
             w_codes.extend(codes[:, i * P : (i + 1) * P] for i in range(2))
             w_scales.extend(scales[:, i * P : (i + 1) * P] for i in range(2))
 
-        def gather_tokens(pair, tag):
-            piece = keep.tile([P, 2 * P], U32, align_bytes=64, name="xw%d" % pair, tag=tag)
-            nc.vector.tensor_copy(piece[:], xw_win[:].indirect(offs_sb[:, pair * 16 : (pair + 1) * 16]))
-            xw.extend(piece[:, i * P : (i + 1) * P] for i in range(2))
+        def gather_tokens(first, last, tag):
+            piece = keep.tile([P, (last - first) * P], U32, align_bytes=64, name="xw%d" % first, tag=tag)
+            nc.vector.tensor_copy(piece[:], xw_win[:].indirect(offs_sb[:, first * 8 : last * 8]))
+            xw.extend(piece[:, i * P : (i + 1) * P] for i in range(last - first))
 
         blocks = S // P
         quantise_w(0)
-        gather_tokens(0, "xw0")
+        gather_tokens(0, 1, "xw0")
+        gather_tokens(1, 2, "xw1")
         quantise_w(1)
-        gather_tokens(1, "w_raw")
+        gather_tokens(2, 4, "w_raw")
 
         h_bf = keep.tile([P, blocks * BANK], BF16, align_bytes=64)
         h_codes, h_scales = [], []
@@ -137,9 +138,12 @@ def tile_picked_zlateq_relu_p_kernel(tc, x_words, x_scales, w1, v_words, v_scale
 
         def finish(a, b):
             best = keep.tile([P, nv], F32, name="best%d_%d" % (a, b))
-            odd = keep.tile([P, nv], F32, name="odd%d_%d" % (a, b))
-            nc.scalar.activation(odd[:], y_acc[a, b][:, 1::2], COPY)
-            nc.vector.tensor_tensor(best[:], y_acc[a, b][:, 0::2], odd[:], MAX)
+            if (a, b) == (0, 0):
+                nc.vector.tensor_reduce(best[:], y_acc[a, b][:].rearrange("p (v d) -> p v d", d=D), mybir.AxisListType.X, MAX)
+            else:
+                odd = keep.tile([P, nv], F32, name="odd%d_%d" % (a, b))
+                nc.scalar.activation(odd[:], y_acc[a, b][:, 1::2], COPY)
+                nc.vector.tensor_tensor(best[:], y_acc[a, b][:, 0::2], odd[:], MAX)
             nc.sync.dma_start(out=out[b * P : (b + 1) * P, a * nv : (a + 1) * nv], in_=best[:])
 
         for b in range(blocks):

@@ -13,7 +13,6 @@ U16 = mybir.dt.uint16
 U8 = mybir.dt.uint8
 FP8X4 = mybir.dt.float8_e4m3fn_x4
 RELU = mybir.ActivationFunctionType.Relu
-COPY = mybir.ActivationFunctionType.Copy
 MAX = mybir.AluOpType.max
 
 P = 128
@@ -63,7 +62,7 @@ def tile_picked_zlateq_relu_p_kernel(tc, x_words, x_scales, w1, v_words, v_scale
 
         def quantise_w(u):
             w_bf = keep.tile([P, 2 * P * PACK], BF16, align_bytes=64, name="w_bf%d" % u)
-            nc.scalar.activation(w_bf[:].rearrange("p (t m j) -> p m j t", t=2, j=PACK), w_src[:, u], COPY)
+            nc.scalar.copy(w_bf[:].rearrange("p (t m j) -> p m j t", t=2, j=PACK), w_src[:, u])
             codes = keep.tile([P, 2 * P], U32, align_bytes=64, name="w_codes%d" % u)
             scales = keep.tile([P, 2 * P], U8, align_bytes=64, name="w_scales%d" % u)
             nc.vector.quantize_mx(out=codes[:].bitcast(FP8X4), scales=scales[:], in_=w_bf[:])
@@ -138,12 +137,9 @@ def tile_picked_zlateq_relu_p_kernel(tc, x_words, x_scales, w1, v_words, v_scale
 
         def finish(a, b):
             best = keep.tile([P, nv], F32, name="best%d_%d" % (a, b))
-            if (a, b) == (0, 0):
-                nc.vector.tensor_reduce(best[:], y_acc[a, b][:].rearrange("p (v d) -> p v d", d=D), mybir.AxisListType.X, MAX)
-            else:
-                odd = keep.tile([P, nv], F32, name="odd%d_%d" % (a, b))
-                nc.scalar.activation(odd[:], y_acc[a, b][:, 1::2], COPY)
-                nc.vector.tensor_tensor(best[:], y_acc[a, b][:, 0::2], odd[:], MAX)
+            odd = keep.tile([P, nv], F32, name="odd%d_%d" % (a, b))
+            nc.scalar.copy(odd[:], y_acc[a, b][:, 1::2])
+            nc.vector.tensor_tensor(best[:], y_acc[a, b][:, 0::2], odd[:], MAX)
             nc.sync.dma_start(out=out[b * P : (b + 1) * P, a * nv : (a + 1) * nv], in_=best[:])
 
         for b in range(blocks):

@@ -18,6 +18,8 @@ MAX = mybir.AluOpType.max
 P = 128
 PACK = 4
 BANK = 512
+ROWS = 16
+TABLE = P - ROWS
 
 
 def tile_picked_zlateq_relu_p_kernel(tc, x_words, x_scales, w1, v_words, v_scales, offs, doc, out):
@@ -25,44 +27,54 @@ def tile_picked_zlateq_relu_p_kernel(tc, x_words, x_scales, w1, v_words, v_scale
     with ExitStack() as ctx:
         keep = ctx.enter_context(tc.tile_pool(name="keep", bufs=1))
         late = ctx.enter_context(tc.tile_pool(name="late", bufs=1))
+        head = ctx.enter_context(tc.tile_pool(name="head", bufs=1))
         psum = ctx.enter_context(tc.psum_pool(name="psum", bufs=8))
 
         offs_sb = keep.tile([P, S // 16], U16)
         doc_sb = keep.tile([P, V // 16], U16)
-        xs_win = keep.tile([P, T], U8, align_bytes=64)
+        xs_win = head.tile([P, T], U8, align_bytes=64, offset=0)
         vs_win = keep.tile([P, G], U8, align_bytes=64)
         xw_win = keep.tile([P, T], U32, align_bytes=64)
-        vw_win = keep.tile([P, G], U32, align_bytes=64)
         w_raw = keep.tile([P, PACK * H], F32, align_bytes=64, tag="w_raw")
-
+        xs = keep.tile([P, S], U8, align_bytes=64)
         vs = keep.tile([P, V], U8, align_bytes=64)
-        nc.vector.memset(xs_win[:].bitcast(I32), 0)
-        nc.vector.memset(vs_win[:96, :].bitcast(I32), 0)
-        nc.vector.memset(vs_win[96:112, :].bitcast(I32), 0)
+
+        for win in (xs_win, vs_win):
+            nc.vector.memset(win[:96, :].bitcast(I32), 0)
+            nc.vector.memset(win[96:TABLE, :].bitcast(I32), 0)
+        nc.vector.memset(xs[:].bitcast(I32), 0)
         nc.vector.memset(vs[:].bitcast(I32), 0)
 
-        nc.sync.dma_start(out=vs_win[112:, :].bitcast(I32), in_=v_scales[0].bitcast(I32))
-        nc.sync.dma_start(doc_sb[:], doc)
+        nc.scalar.dma_start(out=xs_win[TABLE:, :].bitcast(I32), in_=x_scales[0].bitcast(I32))
         nc.sync.dma_start(offs_sb[:], offs)
+        nc.scalar.dma_start(out=vs_win[TABLE:, :].bitcast(I32), in_=v_scales[0].bitcast(I32))
+        nc.sync.dma_start(doc_sb[:], doc)
         nc.sync.dma_start(out=w_raw[:], in_=w1.rearrange("(p j) i -> p (j i)", j=PACK))
-        for r in range(4):
-            nc.sync.dma_start(out=xs_win[r:P:32, :].bitcast(I32), in_=x_scales[0, r:16:4, :].bitcast(I32))
         nc.sync.dma_start(out=xw_win[:].bitcast(I32), in_=x_words[0].rearrange("p n r -> p (n r)").bitcast(I32))
-        nc.sync.dma_start(out=vw_win[:].bitcast(I32), in_=v_words[0].rearrange("p n r -> p (n r)").bitcast(I32))
 
-        xs = keep.tile([P, S], U8, align_bytes=64)
+        def place(rows, plane):
+            for r in range(4):
+                nc.sync.dma_start(out=plane[r:P:32, :].bitcast(I32), in_=rows[TABLE + r : P : 4, :].bitcast(I32))
+
+        xs_rows = keep.tile([P, S], U8, align_bytes=64)
+        nc.vector.tensor_copy(xs_rows[:], xs_win[:].indirect(offs_sb[:]))
+        place(xs_rows, xs)
+        vw_win = head.tile([P, G], U32, align_bytes=64, offset=0)
+        nc.sync.dma_start(out=vw_win[:].bitcast(I32), in_=v_words[0].rearrange("p n r -> p (n r)").bitcast(I32))
         vs_rows = late.tile([P, V], U8, align_bytes=64, offset=1984)
         nc.vector.tensor_copy(vs_rows[:], vs_win[:].indirect(doc_sb[:]))
-        for r in range(4):
-            nc.sync.dma_start(out=vs[r:P:32, :].bitcast(I32), in_=vs_rows[112 + r : P : 4, :].bitcast(I32))
-        nc.vector.tensor_copy(xs[:], xs_win[:].indirect(offs_sb[:]))
+        place(vs_rows, vs)
 
         w_codes, w_scales, xw = [], [], []
         w_src = w_raw[:].rearrange("p (j m u t) -> p u m j t", j=PACK, u=2, t=2)
 
         def quantise_w(u):
             w_bf = keep.tile([P, 2 * P * PACK], BF16, align_bytes=64, name="w_bf%d" % u)
-            nc.scalar.copy(w_bf[:].rearrange("p (t m j) -> p m j t", t=2, j=PACK), w_src[:, u])
+            dst = w_bf[:].rearrange("p (t m j) -> p m j t", t=2, j=PACK)
+            own = P if u == 0 else 96
+            if own < P:
+                nc.vector.tensor_copy(dst[:, own:], w_src[:, u, own:])
+            nc.scalar.copy(dst[:, :own], w_src[:, u, :own])
             codes = keep.tile([P, 2 * P], U32, align_bytes=64, name="w_codes%d" % u)
             scales = keep.tile([P, 2 * P], U8, align_bytes=64, name="w_scales%d" % u)
             nc.vector.quantize_mx(out=codes[:].bitcast(FP8X4), scales=scales[:], in_=w_bf[:])
@@ -75,9 +87,8 @@ def tile_picked_zlateq_relu_p_kernel(tc, x_words, x_scales, w1, v_words, v_scale
             xw.extend(piece[:, i * P : (i + 1) * P] for i in range(last - first))
 
         blocks = S // P
+        gather_tokens(0, 2, "xw0")
         quantise_w(0)
-        gather_tokens(0, 1, "xw0")
-        gather_tokens(1, 2, "xw1")
         quantise_w(1)
         gather_tokens(2, 4, "w_raw")
 

@@ -35,7 +35,7 @@ def tile_picked_zlateq_relu_p_kernel(tc, x_words, x_scales, w1, v_words, v_scale
         xs_win = head.tile([P, T], U8, align_bytes=64, offset=0)
         vs_win = keep.tile([P, G], U8, align_bytes=64)
         xw_win = keep.tile([P, T], U32, align_bytes=64)
-        w_raw = keep.tile([P, PACK * H], F32, align_bytes=64, tag="w_raw")
+        w_raw = late.tile([P, PACK * H], F32, align_bytes=64, offset=4096)
         xs = keep.tile([P, S], U8, align_bytes=64)
         vs = keep.tile([P, V], U8, align_bytes=64)
 
@@ -71,7 +71,7 @@ def tile_picked_zlateq_relu_p_kernel(tc, x_words, x_scales, w1, v_words, v_scale
         def quantise_w(u):
             w_bf = keep.tile([P, 2 * P * PACK], BF16, align_bytes=64, name="w_bf%d" % u)
             dst = w_bf[:].rearrange("p (t m j) -> p m j t", t=2, j=PACK)
-            own = P if u == 0 else 96
+            own = P if u == 0 else 80
             if own < P:
                 nc.vector.tensor_copy(dst[:, own:], w_src[:, u, own:])
             nc.scalar.copy(dst[:, :own], w_src[:, u, :own])
@@ -81,16 +81,16 @@ def tile_picked_zlateq_relu_p_kernel(tc, x_words, x_scales, w1, v_words, v_scale
             w_codes.extend(codes[:, i * P : (i + 1) * P] for i in range(2))
             w_scales.extend(scales[:, i * P : (i + 1) * P] for i in range(2))
 
-        def gather_tokens(first, last, tag):
-            piece = keep.tile([P, (last - first) * P], U32, align_bytes=64, name="xw%d" % first, tag=tag)
+        def gather_tokens(first, last, piece):
             nc.vector.tensor_copy(piece[:], xw_win[:].indirect(offs_sb[:, first * 8 : last * 8]))
             xw.extend(piece[:, i * P : (i + 1) * P] for i in range(last - first))
 
         blocks = S // P
-        gather_tokens(0, 2, "xw0")
+        gather_tokens(0, 1, keep.tile([P, P], U32, align_bytes=64, name="xw0"))
         quantise_w(0)
         quantise_w(1)
-        gather_tokens(2, 4, "w_raw")
+        gather_tokens(1, 2, late.tile([P, P], U32, align_bytes=64, name="xw1", offset=4096))
+        gather_tokens(2, 4, late.tile([P, 2 * P], U32, align_bytes=64, name="xw2", offset=4096 + 512))
 
         h_bf = keep.tile([P, blocks * BANK], BF16, align_bytes=64)
         h_codes, h_scales = [], []
@@ -115,12 +115,13 @@ def tile_picked_zlateq_relu_p_kernel(tc, x_words, x_scales, w1, v_words, v_scale
                 RELU,
             )
 
-        def quantise_h(b):
-            codes = keep.tile([P, P], U32, align_bytes=64, name="h_codes%d" % b)
-            scales = late.tile([P, P], U8, align_bytes=64, name="h_scales%d" % b, offset=2048 + b * P)
-            nc.vector.quantize_mx(out=codes[:].bitcast(FP8X4), scales=scales[:], in_=h_bf[:, b * BANK : (b + 1) * BANK])
-            h_codes.append(codes)
-            h_scales.append(scales)
+        def quantise_h(first, last):
+            width = (last - first) * P
+            codes = keep.tile([P, width], U32, align_bytes=64, name="h_codes%d" % first)
+            scales = late.tile([P, width], U8, align_bytes=64, name="h_scales%d" % first, offset=2048 + first * P)
+            nc.vector.quantize_mx(out=codes[:].bitcast(FP8X4), scales=scales[:], in_=h_bf[:, first * BANK : last * BANK])
+            h_codes.extend(codes[:, i * P : (i + 1) * P] for i in range(last - first))
+            h_scales.extend(scales[:, i * P : (i + 1) * P] for i in range(last - first))
 
         vw = [keep.tile([P, BANK], U32, align_bytes=64, name="vw0"), late.tile([P, BANK], U32, align_bytes=64, name="vw1", offset=0)]
 
@@ -138,8 +139,8 @@ def tile_picked_zlateq_relu_p_kernel(tc, x_words, x_scales, w1, v_words, v_scale
             cols = slice(first - a * BANK, last - a * BANK)
             nc.tensor.matmul_mx(
                 out=y_acc[a, b][:, cols],
-                lhsT=h_codes[b][:].bitcast(FP8X4),
-                lhsT_scale=h_scales[b][:],
+                lhsT=h_codes[b].bitcast(FP8X4),
+                lhsT_scale=h_scales[b],
                 rhs=vw[a][:, cols].bitcast(FP8X4),
                 rhs_scale=vs[:, first:last],
                 start=True,
@@ -156,21 +157,20 @@ def tile_picked_zlateq_relu_p_kernel(tc, x_words, x_scales, w1, v_words, v_scale
         for b in range(blocks):
             project(b)
         gather_docs(0, 512)
-        quantise_h(0)
-        score(0, 0, 512)
+        quantise_h(0, 2)
+        for b in range(2):
+            score(b, 0, 512)
         gather_docs(512, 768)
-        quantise_h(1)
-        score(1, 0, 512)
-        score(0, 512, 768)
-        score(1, 512, 768)
-        quantise_h(2)
-        score(2, 0, 512)
-        score(2, 512, 768)
+        for b in range(2):
+            score(b, 512, 768)
+        for b in range(2, blocks):
+            quantise_h(b, b + 1)
+            score(b, 0, 512)
+        for b in range(2, blocks):
+            score(b, 512, 768)
         gather_docs(768, 1024)
-        for b in range(3):
+        for b in range(blocks):
             score(b, 768, 1024)
-        quantise_h(3)
-        score(3, 0, 512)
-        score(3, 512, 1024)
-        for a, b in ((0, 0), (0, 1), (0, 2), (1, 0), (1, 1), (1, 2), (0, 3), (1, 3)):
-            finish(a, b)
+        for a in range(2):
+            for b in range(blocks):
+                finish(a, b)

@@ -32,7 +32,7 @@ def tile_picked_zlateq_relu_p_kernel(tc, x_words, x_scales, w1, v_words, v_scale
 
         offs_sb = keep.tile([P, S // 16], U16)
         doc_sb = keep.tile([P, V // 16], U16)
-        xs_win = head.tile([P, T], U8, align_bytes=64, offset=0)
+        xs_win = head.tile([P, T], U8, align_bytes=64, offset=4096)
         vs_win = keep.tile([P, G], U8, align_bytes=64)
         xw_win = keep.tile([P, T], U32, align_bytes=64)
         w_raw = late.tile([P, PACK * H], F32, align_bytes=64, offset=4096)
@@ -51,6 +51,9 @@ def tile_picked_zlateq_relu_p_kernel(tc, x_words, x_scales, w1, v_words, v_scale
         nc.sync.dma_start(doc_sb[:], doc)
         nc.sync.dma_start(out=w_raw[:], in_=w1.rearrange("(p j) i -> p (j i)", j=PACK))
         nc.sync.dma_start(out=xw_win[:].bitcast(I32), in_=x_words[0].rearrange("p n r -> p (n r)").bitcast(I32))
+        vw_win = head.tile([P, G], U32, align_bytes=64, offset=0)
+        v_src = v_words[0].rearrange("p n r -> p (n r)").bitcast(I32)
+        nc.sync.dma_start(out=vw_win[:, :512].bitcast(I32), in_=v_src[:, :512])
 
         def place(rows, plane):
             for r in range(4):
@@ -59,8 +62,7 @@ def tile_picked_zlateq_relu_p_kernel(tc, x_words, x_scales, w1, v_words, v_scale
         xs_rows = keep.tile([P, S], U8, align_bytes=64)
         nc.vector.tensor_copy(xs_rows[:], xs_win[:].indirect(offs_sb[:]))
         place(xs_rows, xs)
-        vw_win = head.tile([P, G], U32, align_bytes=64, offset=0)
-        nc.sync.dma_start(out=vw_win[:].bitcast(I32), in_=v_words[0].rearrange("p n r -> p (n r)").bitcast(I32))
+        nc.sync.dma_start(out=vw_win[:, 512:].bitcast(I32), in_=v_src[:, 512:])
         vs_rows = late.tile([P, V], U8, align_bytes=64, offset=1984)
         nc.vector.tensor_copy(vs_rows[:], vs_win[:].indirect(doc_sb[:]))
         place(vs_rows, vs)

@@ -120,7 +120,7 @@ def tile_picked_zlateq_relu_p_kernel(tc, x_words, x_scales, w1, v_words, v_scale
         def quantise_h(first, last):
             width = (last - first) * P
             codes = keep.tile([P, width], U32, align_bytes=64, name="h_codes%d" % first)
-            scales = late.tile([P, width], U8, align_bytes=64, name="h_scales%d" % first, offset=2048 + first * P)
+            scales = late.tile([P, width], U8, align_bytes=64, name="h_scales%d" % first, offset=(2048 + first * P if first < 3 else 16384))
             nc.vector.quantize_mx(out=codes[:].bitcast(FP8X4), scales=scales[:], in_=h_bf[:, first * BANK : last * BANK])
             h_codes.extend(codes[:, i * P : (i + 1) * P] for i in range(last - first))
             h_scales.extend(scales[:, i * P : (i + 1) * P] for i in range(last - first))
@@ -151,7 +151,7 @@ def tile_picked_zlateq_relu_p_kernel(tc, x_words, x_scales, w1, v_words, v_scale
 
         def finish(a, b):
             best = keep.tile([P, nv], F32, name="best%d_%d" % (a, b))
-            odd = keep.tile([P, nv], F32, name="odd%d_%d" % (a, b))
+            odd = late.tile([P, nv], F32, align_bytes=64, name="odd%d_%d" % (a, b), offset=16384 + (a * blocks + b) * 1024)
             nc.scalar.copy(odd[:], y_acc[a, b][:, 1::2])
             nc.vector.tensor_tensor(best[:], y_acc[a, b][:, 0::2], odd[:], MAX)
             nc.sync.dma_start(out=out[b * P : (b + 1) * P, a * nv : (a + 1) * nv], in_=best[:])
@@ -165,14 +165,16 @@ def tile_picked_zlateq_relu_p_kernel(tc, x_words, x_scales, w1, v_words, v_scale
         gather_docs(512, 768)
         for b in range(2):
             score(b, 512, 768)
-        for b in range(2, blocks):
-            quantise_h(b, b + 1)
-            score(b, 0, 512)
-        for b in range(2, blocks):
-            score(b, 512, 768)
+        quantise_h(2, 3)
+        score(2, 0, 512)
+        score(2, 512, 768)
         gather_docs(768, 1024)
-        for b in range(blocks):
+        for b in range(3):
             score(b, 768, 1024)
-        for a in range(2):
-            for b in range(blocks):
-                finish(a, b)
+        finish(0, 0)
+        finish(0, 1)
+        quantise_h(3, 4)
+        score(3, 0, 512)
+        score(3, 512, 1024)
+        for a, b in ((0, 2), (1, 0), (1, 1), (1, 2), (0, 3), (1, 3)):
+            finish(a, b)

@@ -14,12 +14,15 @@ U8 = mybir.dt.uint8
 FP8X4 = mybir.dt.float8_e4m3fn_x4
 RELU = mybir.ActivationFunctionType.Relu
 MAX = mybir.AluOpType.max
+MULT = mybir.AluOpType.mult
+ADD = mybir.AluOpType.add
 
 P = 128
 PACK = 4
 BANK = 512
 ROWS = 16
 TABLE = P - ROWS
+V_TABLE = 48
 
 
 def tile_picked_zlateq_relu_p_kernel(tc, x_words, x_scales, w1, v_words, v_scales, offs, doc, out):
@@ -39,15 +42,16 @@ def tile_picked_zlateq_relu_p_kernel(tc, x_words, x_scales, w1, v_words, v_scale
         xs = keep.tile([P, S], U8, align_bytes=64)
         vs = keep.tile([P, V], U8, align_bytes=64)
 
-        for win in (xs_win, vs_win):
-            nc.vector.memset(win[:96, :].bitcast(I32), 0)
-            nc.vector.memset(win[96:TABLE, :].bitcast(I32), 0)
+        nc.vector.memset(xs_win[:96, :].bitcast(I32), 0)
+        nc.vector.memset(xs_win[96:TABLE, :].bitcast(I32), 0)
+        nc.vector.memset(vs_win[:V_TABLE, :].bitcast(I32), 0)
+        nc.vector.memset(vs_win[V_TABLE + ROWS :, :].bitcast(I32), 0)
         nc.vector.memset(xs[:].bitcast(I32), 0)
         nc.vector.memset(vs[:].bitcast(I32), 0)
 
         nc.scalar.dma_start(out=xs_win[TABLE:, :].bitcast(I32), in_=x_scales[0].bitcast(I32))
         nc.sync.dma_start(offs_sb[:], offs)
-        nc.scalar.dma_start(out=vs_win[TABLE:, :].bitcast(I32), in_=v_scales[0].bitcast(I32))
+        nc.scalar.dma_start(out=vs_win[V_TABLE : V_TABLE + ROWS, :].bitcast(I32), in_=v_scales[0].bitcast(I32))
         nc.sync.dma_start(doc_sb[:], doc)
         nc.sync.dma_start(out=w_raw[:], in_=w1.rearrange("(p j) i -> p (j i)", j=PACK))
         nc.sync.dma_start(out=xw_win[:].bitcast(I32), in_=x_words[0].rearrange("p n r -> p (n r)").bitcast(I32))
@@ -55,17 +59,17 @@ def tile_picked_zlateq_relu_p_kernel(tc, x_words, x_scales, w1, v_words, v_scale
         v_src = v_words[0].rearrange("p n r -> p (n r)").bitcast(I32)
         nc.sync.dma_start(out=vw_win[:, :512].bitcast(I32), in_=v_src[:, :512])
 
-        def place(rows, plane):
+        def place(rows, first, plane):
             for r in range(4):
-                nc.sync.dma_start(out=plane[r:P:32, :].bitcast(I32), in_=rows[TABLE + r : P : 4, :].bitcast(I32))
+                nc.sync.dma_start(out=plane[r:P:32, :].bitcast(I32), in_=rows[first + r : first + ROWS : 4, :].bitcast(I32))
 
         xs_rows = keep.tile([P, S], U8, align_bytes=64)
         nc.vector.tensor_copy(xs_rows[:], xs_win[:].indirect(offs_sb[:]))
-        place(xs_rows, xs)
+        place(xs_rows, TABLE, xs)
         nc.sync.dma_start(out=vw_win[:, 512:].bitcast(I32), in_=v_src[:, 512:])
         vs_rows = late.tile([P, V], U8, align_bytes=64, offset=1984)
         nc.vector.tensor_copy(vs_rows[:], vs_win[:].indirect(doc_sb[:]))
-        place(vs_rows, vs)
+        place(vs_rows, V_TABLE, vs)
 
         w_codes, w_scales, xw = [], [], []
         w_src = w_raw[:].rearrange("p (j m u t) -> p u m j t", j=PACK, u=2, t=2)
@@ -73,9 +77,9 @@ def tile_picked_zlateq_relu_p_kernel(tc, x_words, x_scales, w1, v_words, v_scale
         def quantise_w(u):
             w_bf = keep.tile([P, 2 * P * PACK], BF16, align_bytes=64, name="w_bf%d" % u)
             dst = w_bf[:].rearrange("p (t m j) -> p m j t", t=2, j=PACK)
-            own = P if u == 0 else 80
+            own = P if u == 0 else 56
             if own < P:
-                nc.vector.tensor_copy(dst[:, own:], w_src[:, u, own:])
+                nc.gpsimd.tensor_scalar(dst[:, own:].rearrange("p m j t -> p m t j"), w_src[:, u, own:].rearrange("p m j t -> p m t j"), 1.0, 0.0, MULT, ADD)
             nc.scalar.copy(dst[:, :own], w_src[:, u, :own])
             codes = keep.tile([P, 2 * P], U32, align_bytes=64, name="w_codes%d" % u)
             scales = keep.tile([P, 2 * P], U8, align_bytes=64, name="w_scales%d" % u)

@@ -21,8 +21,10 @@ P = 128
 PACK = 4
 BANK = 512
 ROWS = 16
-TABLE = P - ROWS
+X_TABLE = P - ROWS
 V_TABLE = 48
+V_AHEAD = 512
+SCALAR_COLUMNS = 40
 
 
 def tile_picked_zlateq_relu_p_kernel(tc, x_words, x_scales, w1, v_words, v_scales, offs, doc, out):
@@ -38,26 +40,28 @@ def tile_picked_zlateq_relu_p_kernel(tc, x_words, x_scales, w1, v_words, v_scale
         xs_win = head.tile([P, T], U8, align_bytes=64, offset=4096)
         vs_win = keep.tile([P, G], U8, align_bytes=64)
         xw_win = keep.tile([P, T], U32, align_bytes=64)
-        w_raw = late.tile([P, PACK * H], F32, align_bytes=64, offset=4096)
+        w_raw = [late.tile([P, 2 * H], F32, align_bytes=64, name="w_raw%d" % i, offset=8192 - 4096 * i) for i in range(2)]
         xs = keep.tile([P, S], U8, align_bytes=64)
         vs = keep.tile([P, V], U8, align_bytes=64)
 
         nc.vector.memset(xs_win[:96, :].bitcast(I32), 0)
-        nc.vector.memset(xs_win[96:TABLE, :].bitcast(I32), 0)
+        nc.vector.memset(xs_win[96:X_TABLE, :].bitcast(I32), 0)
         nc.vector.memset(vs_win[:V_TABLE, :].bitcast(I32), 0)
         nc.vector.memset(vs_win[V_TABLE + ROWS :, :].bitcast(I32), 0)
         nc.vector.memset(xs[:].bitcast(I32), 0)
         nc.vector.memset(vs[:].bitcast(I32), 0)
 
-        nc.scalar.dma_start(out=xs_win[TABLE:, :].bitcast(I32), in_=x_scales[0].bitcast(I32))
+        nc.scalar.dma_start(out=xs_win[X_TABLE:, :].bitcast(I32), in_=x_scales[0].bitcast(I32))
         nc.sync.dma_start(offs_sb[:], offs)
         nc.scalar.dma_start(out=vs_win[V_TABLE : V_TABLE + ROWS, :].bitcast(I32), in_=v_scales[0].bitcast(I32))
         nc.sync.dma_start(doc_sb[:], doc)
-        nc.sync.dma_start(out=w_raw[:], in_=w1.rearrange("(p j) i -> p (j i)", j=PACK))
+        w_rows = w1.rearrange("(p j) i -> p (j i)", j=PACK)
+        for i in range(2):
+            nc.sync.dma_start(out=w_raw[i][:], in_=w_rows[:, i * 2 * H : (i + 1) * 2 * H])
         nc.sync.dma_start(out=xw_win[:].bitcast(I32), in_=x_words[0].rearrange("p n r -> p (n r)").bitcast(I32))
         vw_win = head.tile([P, G], U32, align_bytes=64, offset=0)
         v_src = v_words[0].rearrange("p n r -> p (n r)").bitcast(I32)
-        nc.sync.dma_start(out=vw_win[:, :512].bitcast(I32), in_=v_src[:, :512])
+        nc.sync.dma_start(out=vw_win[:, :V_AHEAD].bitcast(I32), in_=v_src[:, :V_AHEAD])
 
         def place(rows, first, plane):
             for r in range(4):
@@ -65,25 +69,27 @@ def tile_picked_zlateq_relu_p_kernel(tc, x_words, x_scales, w1, v_words, v_scale
 
         xs_rows = keep.tile([P, S], U8, align_bytes=64)
         nc.vector.tensor_copy(xs_rows[:], xs_win[:].indirect(offs_sb[:]))
-        place(xs_rows, TABLE, xs)
-        nc.sync.dma_start(out=vw_win[:, 512:].bitcast(I32), in_=v_src[:, 512:])
+        place(xs_rows, X_TABLE, xs)
+        nc.sync.dma_start(out=vw_win[:, V_AHEAD:].bitcast(I32), in_=v_src[:, V_AHEAD:])
         vs_rows = late.tile([P, V], U8, align_bytes=64, offset=1984)
         nc.vector.tensor_copy(vs_rows[:], vs_win[:].indirect(doc_sb[:]))
         place(vs_rows, V_TABLE, vs)
 
         w_codes, w_scales, xw = [], [], []
-        w_src = w_raw[:].rearrange("p (j m u t) -> p u m j t", j=PACK, u=2, t=2)
+        w_bf = [keep.tile([P, 2 * P * PACK], BF16, align_bytes=64, name="w_bf%d" % u) for u in range(2)]
+
+        def round_w(i):
+            src = w_raw[i][:].rearrange("p (j m u t) -> p u m j t", j=2, u=2, t=2)
+            dst = [w_bf[u][:].rearrange("p (t m j) -> p m j t", t=2, j=PACK)[:, :, 2 * i : 2 * i + 2] for u in range(2)]
+            own = SCALAR_COLUMNS
+            nc.gpsimd.tensor_scalar(dst[1][:, own:].rearrange("p m j t -> p m t j"), src[:, 1, own:].rearrange("p m j t -> p m t j"), 1.0, 0.0, MULT, ADD)
+            nc.scalar.copy(dst[0], src[:, 0])
+            nc.scalar.copy(dst[1][:, :own], src[:, 1, :own])
 
         def quantise_w(u):
-            w_bf = keep.tile([P, 2 * P * PACK], BF16, align_bytes=64, name="w_bf%d" % u)
-            dst = w_bf[:].rearrange("p (t m j) -> p m j t", t=2, j=PACK)
-            own = P if u == 0 else 56
-            if own < P:
-                nc.gpsimd.tensor_scalar(dst[:, own:].rearrange("p m j t -> p m t j"), w_src[:, u, own:].rearrange("p m j t -> p m t j"), 1.0, 0.0, MULT, ADD)
-            nc.scalar.copy(dst[:, :own], w_src[:, u, :own])
             codes = keep.tile([P, 2 * P], U32, align_bytes=64, name="w_codes%d" % u)
             scales = keep.tile([P, 2 * P], U8, align_bytes=64, name="w_scales%d" % u)
-            nc.vector.quantize_mx(out=codes[:].bitcast(FP8X4), scales=scales[:], in_=w_bf[:])
+            nc.vector.quantize_mx(out=codes[:].bitcast(FP8X4), scales=scales[:], in_=w_bf[u][:])
             w_codes.extend(codes[:, i * P : (i + 1) * P] for i in range(2))
             w_scales.extend(scales[:, i * P : (i + 1) * P] for i in range(2))
 
@@ -92,8 +98,10 @@ def tile_picked_zlateq_relu_p_kernel(tc, x_words, x_scales, w1, v_words, v_scale
             xw.extend(piece[:, i * P : (i + 1) * P] for i in range(last - first))
 
         blocks = S // P
-        gather_tokens(0, 1, keep.tile([P, P], U32, align_bytes=64, name="xw0"))
+        round_w(0)
+        round_w(1)
         quantise_w(0)
+        gather_tokens(0, 1, keep.tile([P, P], U32, align_bytes=64, name="xw0"))
         quantise_w(1)
         gather_tokens(1, 2, late.tile([P, P], U32, align_bytes=64, name="xw1", offset=4096))
         gather_tokens(2, 4, late.tile([P, 2 * P], U32, align_bytes=64, name="xw2", offset=4096 + 512))
@@ -121,19 +129,20 @@ def tile_picked_zlateq_relu_p_kernel(tc, x_words, x_scales, w1, v_words, v_scale
                 RELU,
             )
 
-        def quantise_h(first, last):
+        def quantise_h(first, last, offset):
             width = (last - first) * P
             codes = keep.tile([P, width], U32, align_bytes=64, name="h_codes%d" % first)
-            scales = late.tile([P, width], U8, align_bytes=64, name="h_scales%d" % first, offset=(2048 + first * P if first < 3 else 16384))
+            scales = late.tile([P, width], U8, align_bytes=64, name="h_scales%d" % first, offset=offset)
             nc.vector.quantize_mx(out=codes[:].bitcast(FP8X4), scales=scales[:], in_=h_bf[:, first * BANK : last * BANK])
             h_codes.extend(codes[:, i * P : (i + 1) * P] for i in range(last - first))
             h_scales.extend(scales[:, i * P : (i + 1) * P] for i in range(last - first))
 
-        vw = [keep.tile([P, BANK], U32, align_bytes=64, name="vw0"), late.tile([P, BANK], U32, align_bytes=64, name="vw1", offset=0)]
+        vw = {}
 
-        def gather_docs(first, last):
-            a = first // BANK
-            nc.vector.tensor_copy(vw[a][:, first - a * BANK : last - a * BANK], vw_win[:].indirect(doc_sb[:, first // 16 : last // 16]))
+        def gather_docs(first, last, offset):
+            piece = late.tile([P, last - first], U32, align_bytes=64, name="vw%d" % first, offset=offset)
+            nc.vector.tensor_copy(piece[:], vw_win[:].indirect(doc_sb[:, first // 16 : last // 16]))
+            vw[first] = piece
 
         nv = BANK // D
         y_acc = {}
@@ -142,12 +151,11 @@ def tile_picked_zlateq_relu_p_kernel(tc, x_words, x_scales, w1, v_words, v_scale
             a = first // BANK
             if (a, b) not in y_acc:
                 y_acc[a, b] = psum.tile([P, BANK], F32, tag="bank", name="y_acc%d_%d" % (a, b))
-            cols = slice(first - a * BANK, last - a * BANK)
             nc.tensor.matmul_mx(
-                out=y_acc[a, b][:, cols],
+                out=y_acc[a, b][:, first - a * BANK : last - a * BANK],
                 lhsT=h_codes[b].bitcast(FP8X4),
                 lhsT_scale=h_scales[b],
-                rhs=vw[a][:, cols].bitcast(FP8X4),
+                rhs=vw[first][:].bitcast(FP8X4),
                 rhs_scale=vs[:, first:last],
                 start=True,
                 stop=True,
@@ -162,23 +170,21 @@ def tile_picked_zlateq_relu_p_kernel(tc, x_words, x_scales, w1, v_words, v_scale
 
         for b in range(blocks):
             project(b)
-        gather_docs(0, 512)
-        quantise_h(0, 2)
-        for b in range(2):
+        quantise_h(0, 1, 32768)
+        gather_docs(0, 512, 36864)
+        score(0, 0, 512)
+        quantise_h(1, 3, 2048)
+        for b in range(1, 3):
             score(b, 0, 512)
-        gather_docs(512, 768)
-        for b in range(2):
-            score(b, 512, 768)
-        quantise_h(2, 3)
-        score(2, 0, 512)
-        score(2, 512, 768)
-        gather_docs(768, 1024)
+        gather_docs(512, 768, 1024)
         for b in range(3):
-            score(b, 768, 1024)
-        finish(0, 0)
-        finish(0, 1)
-        quantise_h(3, 4)
+            score(b, 512, 768)
+        quantise_h(3, 4, 2304)
         score(3, 0, 512)
-        score(3, 512, 1024)
-        for a, b in ((0, 2), (1, 0), (1, 1), (1, 2), (0, 3), (1, 3)):
-            finish(a, b)
+        score(3, 512, 768)
+        gather_docs(768, 1024, 2432)
+        for b in range(blocks):
+            score(b, 768, 1024)
+        for a in range(2):
+            for b in range(blocks):
+                finish(a, b)

@@ -37,12 +37,12 @@ def tile_picked_zlateq_relu_p_kernel(tc, x_words, x_scales, w1, v_words, v_scale
 
         offs_sb = keep.tile([P, S // 16], U16)
         doc_sb = keep.tile([P, V // 16], U16)
-        xs_win = head.tile([P, T], U8, align_bytes=64, offset=4096)
-        vs_win = keep.tile([P, G], U8, align_bytes=64)
-        xw_win = keep.tile([P, T], U32, align_bytes=64)
-        w_raw = [late.tile([P, 2 * H], F32, align_bytes=64, name="w_raw%d" % i, offset=8192 - 4096 * i) for i in range(2)]
-        xs = keep.tile([P, S], U8, align_bytes=64)
-        vs = keep.tile([P, V], U8, align_bytes=64)
+        xs_win = head.tile([P, T], U8, align_bytes=256, offset=4096)
+        vs_win = keep.tile([P, G], U8, align_bytes=256)
+        xw_win = keep.tile([P, T], U32, align_bytes=256)
+        w_raw = [late.tile([P, 2 * H], F32, align_bytes=256, name="w_raw%d" % i, offset=8192 - 4096 * i) for i in range(2)]
+        xs = keep.tile([P, S], U8, align_bytes=256)
+        vs = keep.tile([P, V], U8, align_bytes=256)
 
         nc.vector.memset(xs_win[:96, :].bitcast(I32), 0)
         nc.vector.memset(xs_win[96:X_TABLE, :].bitcast(I32), 0)
@@ -59,7 +59,7 @@ def tile_picked_zlateq_relu_p_kernel(tc, x_words, x_scales, w1, v_words, v_scale
         for i in range(2):
             nc.sync.dma_start(out=w_raw[i][:], in_=w_rows[:, i * 2 * H : (i + 1) * 2 * H])
         nc.sync.dma_start(out=xw_win[:].bitcast(I32), in_=x_words[0].rearrange("p n r -> p (n r)").bitcast(I32))
-        vw_win = head.tile([P, G], U32, align_bytes=64, offset=0)
+        vw_win = head.tile([P, G], U32, align_bytes=256, offset=0)
         v_src = v_words[0].rearrange("p n r -> p (n r)").bitcast(I32)
         nc.sync.dma_start(out=vw_win[:, :V_AHEAD].bitcast(I32), in_=v_src[:, :V_AHEAD])
 
@@ -67,11 +67,11 @@ def tile_picked_zlateq_relu_p_kernel(tc, x_words, x_scales, w1, v_words, v_scale
             for r in range(4):
                 nc.sync.dma_start(out=plane[r:P:32, :].bitcast(I32), in_=rows[first + r : first + ROWS : 4, :].bitcast(I32))
 
-        xs_rows = keep.tile([P, S], U8, align_bytes=64)
+        xs_rows = keep.tile([P, S], U8, align_bytes=256)
         nc.vector.tensor_copy(xs_rows[:], xs_win[:].indirect(offs_sb[:]))
         place(xs_rows, X_TABLE, xs)
         nc.sync.dma_start(out=vw_win[:, V_AHEAD:].bitcast(I32), in_=v_src[:, V_AHEAD:])
-        vs_rows = late.tile([P, V], U8, align_bytes=64, offset=1984)
+        vs_rows = late.tile([P, V], U8, align_bytes=256, offset=1792)
         nc.vector.tensor_copy(vs_rows[:], vs_win[:].indirect(doc_sb[:]))
         place(vs_rows, V_TABLE, vs)
 
@@ -146,6 +146,7 @@ def tile_picked_zlateq_relu_p_kernel(tc, x_words, x_scales, w1, v_words, v_scale
 
         nv = BANK // D
         y_acc = {}
+        pair = []
 
         def score(b, first, last):
             a = first // BANK
@@ -162,29 +163,38 @@ def tile_picked_zlateq_relu_p_kernel(tc, x_words, x_scales, w1, v_words, v_scale
             )
 
         def finish(a, b):
-            best = keep.tile([P, nv], F32, name="best%d_%d" % (a, b))
+            if (a, b) == (0, 0):
+                pair.append(keep.tile([P, 2, nv], F32, align_bytes=256, name="best_pair"))
+            joint = a == 0 and b < 2
+            best = pair[0][:, b] if joint else keep.tile([P, nv], F32, align_bytes=256, name="best%d_%d" % (a, b))[:]
             odd = late.tile([P, nv], F32, align_bytes=64, name="odd%d_%d" % (a, b), offset=16384 + (a * blocks + b) * 1024)
             nc.scalar.copy(odd[:], y_acc[a, b][:, 1::2])
-            nc.vector.tensor_tensor(best[:], y_acc[a, b][:, 0::2], odd[:], MAX)
-            nc.sync.dma_start(out=out[b * P : (b + 1) * P, a * nv : (a + 1) * nv], in_=best[:])
+            nc.vector.tensor_tensor(best, y_acc[a, b][:, 0::2], odd[:], MAX)
+            if not joint:
+                nc.sync.dma_start(out=out[b * P : (b + 1) * P, a * nv : (a + 1) * nv], in_=best)
+            elif b == 1:
+                nc.sync.dma_start(out=out[: 2 * P, :nv].rearrange("(b p) v -> p b v", b=2), in_=pair[0][:])
 
         for b in range(blocks):
             project(b)
-        quantise_h(0, 1, 32768)
         gather_docs(0, 512, 36864)
-        score(0, 0, 512)
-        quantise_h(1, 3, 2048)
-        for b in range(1, 3):
+        quantise_h(0, 2, 2048)
+        for b in range(2):
             score(b, 0, 512)
         gather_docs(512, 768, 1024)
-        for b in range(3):
+        for b in range(2):
             score(b, 512, 768)
-        quantise_h(3, 4, 2304)
+        quantise_h(2, 3, 2304)
+        score(2, 0, 512)
+        score(2, 512, 768)
+        gather_docs(768, 1024, 2432)
+        for b in range(3):
+            score(b, 768, 1024)
+        finish(0, 0)
+        finish(0, 1)
+        quantise_h(3, 4, 16384)
         score(3, 0, 512)
         score(3, 512, 768)
-        gather_docs(768, 1024, 2432)
-        for b in range(blocks):
-            score(b, 768, 1024)
-        for a in range(2):
-            for b in range(blocks):
-                finish(a, b)
+        score(3, 768, 1024)
+        for a, b in ((0, 2), (1, 0), (1, 1), (1, 2), (0, 3), (1, 3)):
+            finish(a, b)

@@ -35,8 +35,8 @@ def tile_picked_zlateq_relu_p_kernel(tc, x_words, x_scales, w1, v_words, v_scale
         head = ctx.enter_context(tc.tile_pool(name="head", bufs=1))
         psum = ctx.enter_context(tc.psum_pool(name="psum", bufs=8))
 
-        offs_sb = keep.tile([P, S // 16], U16)
-        doc_sb = keep.tile([P, V // 16], U16)
+        offs_sb = keep.tile([P, S // 16], U16, align_bytes=256)
+        doc_sb = keep.tile([P, V // 16], U16, align_bytes=256)
         xs_win = head.tile([P, T], U8, align_bytes=256, offset=4096)
         vs_win = keep.tile([P, G], U8, align_bytes=256)
         xw_win = keep.tile([P, T], U32, align_bytes=256)
@@ -44,12 +44,11 @@ def tile_picked_zlateq_relu_p_kernel(tc, x_words, x_scales, w1, v_words, v_scale
         xs = keep.tile([P, S], U8, align_bytes=256)
         vs = keep.tile([P, V], U8, align_bytes=256)
 
-        nc.vector.memset(xs_win[:96, :].bitcast(I32), 0)
-        nc.vector.memset(xs_win[96:X_TABLE, :].bitcast(I32), 0)
+        nc.vector.memset(xs_win[:X_TABLE, :].bitcast(I32), 0)
         nc.vector.memset(vs_win[:V_TABLE, :].bitcast(I32), 0)
-        nc.vector.memset(vs_win[V_TABLE + ROWS :, :].bitcast(I32), 0)
+        nc.gpsimd.memset(vs_win[V_TABLE + ROWS :, :].bitcast(I32), 0)
         nc.vector.memset(xs[:].bitcast(I32), 0)
-        nc.vector.memset(vs[:].bitcast(I32), 0)
+        nc.gpsimd.memset(vs[:].bitcast(I32), 0)
 
         nc.scalar.dma_start(out=xs_win[X_TABLE:, :].bitcast(I32), in_=x_scales[0].bitcast(I32))
         nc.sync.dma_start(offs_sb[:], offs)
@@ -76,7 +75,7 @@ def tile_picked_zlateq_relu_p_kernel(tc, x_words, x_scales, w1, v_words, v_scale
         place(vs_rows, V_TABLE, vs)
 
         w_codes, w_scales, xw = [], [], []
-        w_bf = [keep.tile([P, 2 * P * PACK], BF16, align_bytes=64, name="w_bf%d" % u) for u in range(2)]
+        w_bf = [keep.tile([P, 2 * P * PACK], BF16, align_bytes=256, name="w_bf%d" % u) for u in range(2)]
 
         def round_w(i):
             src = w_raw[i][:].rearrange("p (j m u t) -> p u m j t", j=2, u=2, t=2)
@@ -87,8 +86,8 @@ def tile_picked_zlateq_relu_p_kernel(tc, x_words, x_scales, w1, v_words, v_scale
             nc.scalar.copy(dst[1][:, :own], src[:, 1, :own])
 
         def quantise_w(u):
-            codes = keep.tile([P, 2 * P], U32, align_bytes=64, name="w_codes%d" % u)
-            scales = keep.tile([P, 2 * P], U8, align_bytes=64, name="w_scales%d" % u)
+            codes = keep.tile([P, 2 * P], U32, align_bytes=256, name="w_codes%d" % u)
+            scales = keep.tile([P, 2 * P], U8, align_bytes=256, name="w_scales%d" % u)
             nc.vector.quantize_mx(out=codes[:].bitcast(FP8X4), scales=scales[:], in_=w_bf[u][:])
             w_codes.extend(codes[:, i * P : (i + 1) * P] for i in range(2))
             w_scales.extend(scales[:, i * P : (i + 1) * P] for i in range(2))
@@ -101,12 +100,12 @@ def tile_picked_zlateq_relu_p_kernel(tc, x_words, x_scales, w1, v_words, v_scale
         round_w(0)
         round_w(1)
         quantise_w(0)
-        gather_tokens(0, 1, keep.tile([P, P], U32, align_bytes=64, name="xw0"))
+        gather_tokens(0, 1, keep.tile([P, P], U32, align_bytes=256, name="xw0"))
         quantise_w(1)
         gather_tokens(1, 2, late.tile([P, P], U32, align_bytes=64, name="xw1", offset=4096))
         gather_tokens(2, 4, late.tile([P, 2 * P], U32, align_bytes=64, name="xw2", offset=4096 + 512))
 
-        h_bf = keep.tile([P, blocks * BANK], BF16, align_bytes=64)
+        h_bf = keep.tile([P, blocks * BANK], BF16, align_bytes=256)
         h_codes, h_scales = [], []
 
         def project(b):
@@ -131,7 +130,7 @@ def tile_picked_zlateq_relu_p_kernel(tc, x_words, x_scales, w1, v_words, v_scale
 
         def quantise_h(first, last, offset):
             width = (last - first) * P
-            codes = keep.tile([P, width], U32, align_bytes=64, name="h_codes%d" % first)
+            codes = keep.tile([P, width], U32, align_bytes=256, name="h_codes%d" % first)
             scales = late.tile([P, width], U8, align_bytes=64, name="h_scales%d" % first, offset=offset)
             nc.vector.quantize_mx(out=codes[:].bitcast(FP8X4), scales=scales[:], in_=h_bf[:, first * BANK : last * BANK])
             h_codes.extend(codes[:, i * P : (i + 1) * P] for i in range(last - first))
@@ -187,7 +186,7 @@ def tile_picked_zlateq_relu_p_kernel(tc, x_words, x_scales, w1, v_words, v_scale
         quantise_h(2, 3, 2304)
         score(2, 0, 512)
         score(2, 512, 768)
-        gather_docs(768, 1024, 2432)
+        gather_docs(768, 1024, 2560)
         for b in range(3):
             score(b, 768, 1024)
         finish(0, 0)

@@ -23,8 +23,7 @@ BANK = 512
 ROWS = 16
 X_TABLE = P - ROWS
 V_TABLE = 48
-V_AHEAD = 512
-SCALAR_COLUMNS = 40
+V_AHEAD = 384
 
 
 def tile_picked_zlateq_relu_p_kernel(tc, x_words, x_scales, w1, v_words, v_scales, offs, doc, out):
@@ -80,17 +79,20 @@ def tile_picked_zlateq_relu_p_kernel(tc, x_words, x_scales, w1, v_words, v_scale
         def round_w(i):
             src = w_raw[i][:].rearrange("p (j m u t) -> p u m j t", j=2, u=2, t=2)
             dst = [w_bf[u][:].rearrange("p (t m j) -> p m j t", t=2, j=PACK)[:, :, 2 * i : 2 * i + 2] for u in range(2)]
-            own = SCALAR_COLUMNS
-            nc.gpsimd.tensor_scalar(dst[1][:, own:].rearrange("p m j t -> p m t j"), src[:, 1, own:].rearrange("p m j t -> p m t j"), 1.0, 0.0, MULT, ADD)
-            nc.scalar.copy(dst[0], src[:, 0])
-            nc.scalar.copy(dst[1][:, :own], src[:, 1, :own])
+            nc.gpsimd.tensor_scalar(dst[1].rearrange("p m j t -> p m t j"), src[:, 1].rearrange("p m j t -> p m t j"), 1.0, 0.0, MULT, ADD)
+            if i == 0:
+                nc.scalar.copy(dst[0], src[:, 0])
+            else:
+                for t in range(2):
+                    nc.scalar.copy(dst[0][:, :, :, t], src[:, 0, :, :, t])
 
-        def quantise_w(u):
-            codes = keep.tile([P, 2 * P], U32, align_bytes=256, name="w_codes%d" % u)
-            scales = keep.tile([P, 2 * P], U8, align_bytes=256, name="w_scales%d" % u)
-            nc.vector.quantize_mx(out=codes[:].bitcast(FP8X4), scales=scales[:], in_=w_bf[u][:])
-            w_codes.extend(codes[:, i * P : (i + 1) * P] for i in range(2))
-            w_scales.extend(scales[:, i * P : (i + 1) * P] for i in range(2))
+        def quantise_w(t):
+            pool, place_at = (keep, {}) if t == 0 else (late, {"offset": 4096 + 1536 + t * 512})
+            codes = pool.tile([P, P], U32, align_bytes=256, name="w_codes%d" % t, **place_at)
+            scales = keep.tile([P, P], U8, align_bytes=256, name="w_scales%d" % t)
+            nc.vector.quantize_mx(out=codes[:].bitcast(FP8X4), scales=scales[:], in_=w_bf[t // 2][:, (t % 2) * BANK : (t % 2 + 1) * BANK])
+            w_codes.append(codes[:])
+            w_scales.append(scales[:])
 
         def gather_tokens(first, last, piece):
             nc.vector.tensor_copy(piece[:], xw_win[:].indirect(offs_sb[:, first * 8 : last * 8]))
@@ -101,7 +103,8 @@ def tile_picked_zlateq_relu_p_kernel(tc, x_words, x_scales, w1, v_words, v_scale
         round_w(1)
         quantise_w(0)
         gather_tokens(0, 1, keep.tile([P, P], U32, align_bytes=256, name="xw0"))
-        quantise_w(1)
+        for t in range(1, PACK):
+            quantise_w(t)
         gather_tokens(1, 2, late.tile([P, P], U32, align_bytes=64, name="xw1", offset=4096))
         gather_tokens(2, 4, late.tile([P, 2 * P], U32, align_bytes=64, name="xw2", offset=4096 + 512))
 

from contextlib import ExitStack

import concourse.mybir as mybir

K, T, S, D, H, V, G = 512, 1024, 512, 2, 512, 1024, 2048
FLOPS = 2 * K * H * S + 2 * H * S * V

F32 = mybir.dt.float32
BF16 = mybir.dt.bfloat16
I32 = mybir.dt.int32
U32 = mybir.dt.uint32
U16 = mybir.dt.uint16
U8 = mybir.dt.uint8
FP8X4 = mybir.dt.float8_e4m3fn_x4
RELU = mybir.ActivationFunctionType.Relu
MAX = mybir.AluOpType.max
MULT = mybir.AluOpType.mult
ADD = mybir.AluOpType.add

P = 128
PACK = 4
BANK = 512
ROWS = 16
X_TABLE = P - ROWS
V_TABLE = 48
V_AHEAD = 384


def tile_picked_zlateq_relu_p_kernel(tc, x_words, x_scales, w1, v_words, v_scales, offs, doc, out):
    nc = tc.nc
    with ExitStack() as ctx:
        keep = ctx.enter_context(tc.tile_pool(name="keep", bufs=1))
        late = ctx.enter_context(tc.tile_pool(name="late", bufs=1))
        head = ctx.enter_context(tc.tile_pool(name="head", bufs=1))
        psum = ctx.enter_context(tc.psum_pool(name="psum", bufs=8))

        offs_sb = keep.tile([P, S // 16], U16, align_bytes=256)
        doc_sb = keep.tile([P, V // 16], U16, align_bytes=256)
        xs_win = head.tile([P, T], U8, align_bytes=256, offset=4096)
        vs_win = keep.tile([P, G], U8, align_bytes=256)
        xw_win = keep.tile([P, T], U32, align_bytes=256)
        w_raw = [late.tile([P, 2 * H], F32, align_bytes=256, name="w_raw%d" % i, offset=8192 - 4096 * i) for i in range(2)]
        xs = keep.tile([P, S], U8, align_bytes=256)
        vs = keep.tile([P, V], U8, align_bytes=256)

        nc.vector.memset(xs_win[:X_TABLE, :].bitcast(I32), 0)
        nc.vector.memset(vs_win[:V_TABLE, :].bitcast(I32), 0)
        nc.gpsimd.memset(vs_win[V_TABLE + ROWS :, :].bitcast(I32), 0)
        nc.vector.memset(xs[:].bitcast(I32), 0)
        nc.gpsimd.memset(vs[:].bitcast(I32), 0)

        nc.scalar.dma_start(out=xs_win[X_TABLE:, :].bitcast(I32), in_=x_scales[0].bitcast(I32))
        nc.sync.dma_start(offs_sb[:], offs)
        nc.scalar.dma_start(out=vs_win[V_TABLE : V_TABLE + ROWS, :].bitcast(I32), in_=v_scales[0].bitcast(I32))
        nc.sync.dma_start(doc_sb[:], doc)
        w_rows = w1.rearrange("(p j) i -> p (j i)", j=PACK)
        for i in range(2):
            nc.sync.dma_start(out=w_raw[i][:], in_=w_rows[:, i * 2 * H : (i + 1) * 2 * H])
        nc.sync.dma_start(out=xw_win[:].bitcast(I32), in_=x_words[0].rearrange("p n r -> p (n r)").bitcast(I32))
        vw_win = head.tile([P, G], U32, align_bytes=256, offset=0)
        v_src = v_words[0].rearrange("p n r -> p (n r)").bitcast(I32)
        nc.sync.dma_start(out=vw_win[:, :V_AHEAD].bitcast(I32), in_=v_src[:, :V_AHEAD])

        def place(rows, first, plane):
            for r in range(4):
                nc.sync.dma_start(out=plane[r:P:32, :].bitcast(I32), in_=rows[first + r : first + ROWS : 4, :].bitcast(I32))

        xs_rows = keep.tile([P, S], U8, align_bytes=256)
        nc.vector.tensor_copy(xs_rows[:], xs_win[:].indirect(offs_sb[:]))
        place(xs_rows, X_TABLE, xs)
        nc.sync.dma_start(out=vw_win[:, V_AHEAD:].bitcast(I32), in_=v_src[:, V_AHEAD:])
        vs_rows = late.tile([P, V], U8, align_bytes=256, offset=1792)
        nc.vector.tensor_copy(vs_rows[:], vs_win[:].indirect(doc_sb[:]))
        place(vs_rows, V_TABLE, vs)

        w_codes, w_scales, xw = [], [], []
        w_bf = [keep.tile([P, 2 * P * PACK], BF16, align_bytes=256, name="w_bf%d" % u) for u in range(2)]

        def round_w(i):
            src = w_raw[i][:].rearrange("p (j m u t) -> p u m j t", j=2, u=2, t=2)
            dst = [w_bf[u][:].rearrange("p (t m j) -> p m j t", t=2, j=PACK)[:, :, 2 * i : 2 * i + 2] for u in range(2)]
            nc.gpsimd.tensor_scalar(dst[1].rearrange("p m j t -> p m t j"), src[:, 1].rearrange("p m j t -> p m t j"), 1.0, 0.0, MULT, ADD)
            if i == 0:
                nc.scalar.copy(dst[0], src[:, 0])
            else:
                for t in range(2):
                    nc.scalar.copy(dst[0][:, :, :, t], src[:, 0, :, :, t])

        def quantise_w(t):
            pool, place_at = (keep, {}) if t == 0 else (late, {"offset": 4096 + 1536 + t * 512})
            codes = pool.tile([P, P], U32, align_bytes=256, name="w_codes%d" % t, **place_at)
            scales = keep.tile([P, P], U8, align_bytes=256, name="w_scales%d" % t)
            nc.vector.quantize_mx(out=codes[:].bitcast(FP8X4), scales=scales[:], in_=w_bf[t // 2][:, (t % 2) * BANK : (t % 2 + 1) * BANK])
            w_codes.append(codes[:])
            w_scales.append(scales[:])

        def gather_tokens(first, last, piece):
            nc.vector.tensor_copy(piece[:], xw_win[:].indirect(offs_sb[:, first * 8 : last * 8]))
            xw.extend(piece[:, i * P : (i + 1) * P] for i in range(last - first))

        blocks = S // P
        round_w(0)
        round_w(1)
        quantise_w(0)
        gather_tokens(0, 1, keep.tile([P, P], U32, align_bytes=256, name="xw0"))
        for t in range(1, PACK):
            quantise_w(t)
        gather_tokens(1, 2, late.tile([P, P], U32, align_bytes=64, name="xw1", offset=4096))
        gather_tokens(2, 4, late.tile([P, 2 * P], U32, align_bytes=64, name="xw2", offset=4096 + 512))

        h_bf = keep.tile([P, blocks * BANK], BF16, align_bytes=256)
        h_codes, h_scales = [], []

        def project(b):
            h_acc = psum.tile([P, BANK], F32, tag="bank", name="h_acc%d" % b)
            cols = slice(b * P, (b + 1) * P)
            for t in range(PACK):
                ch = slice(t * P, (t + 1) * P)
                nc.tensor.matmul_mx(
                    out=h_acc[:, ch],
                    lhsT=w_codes[t].bitcast(FP8X4),
                    lhsT_scale=w_scales[t],
                    rhs=xw[b].bitcast(FP8X4),
                    rhs_scale=xs[:, cols],
                    start=True,
                    stop=True,
                )
            nc.scalar.activation(
                h_bf[:, b * BANK : (b + 1) * BANK].rearrange("p (n t) -> p n t", t=PACK),
                h_acc[:].rearrange("p (t n) -> p n t", t=PACK),
                RELU,
            )

        def quantise_h(first, last, offset):
            width = (last - first) * P
            codes = keep.tile([P, width], U32, align_bytes=256, name="h_codes%d" % first)
            scales = late.tile([P, width], U8, align_bytes=64, name="h_scales%d" % first, offset=offset)
            nc.vector.quantize_mx(out=codes[:].bitcast(FP8X4), scales=scales[:], in_=h_bf[:, first * BANK : last * BANK])
            h_codes.extend(codes[:, i * P : (i + 1) * P] for i in range(last - first))
            h_scales.extend(scales[:, i * P : (i + 1) * P] for i in range(last - first))

        vw = {}

        def gather_docs(first, last, offset):
            piece = late.tile([P, last - first], U32, align_bytes=64, name="vw%d" % first, offset=offset)
            nc.vector.tensor_copy(piece[:], vw_win[:].indirect(doc_sb[:, first // 16 : last // 16]))
            vw[first] = piece

        nv = BANK // D
        y_acc = {}
        pair = []

        def score(b, first, last):
            a = first // BANK
            if (a, b) not in y_acc:
                y_acc[a, b] = psum.tile([P, BANK], F32, tag="bank", name="y_acc%d_%d" % (a, b))
            nc.tensor.matmul_mx(
                out=y_acc[a, b][:, first - a * BANK : last - a * BANK],
                lhsT=h_codes[b].bitcast(FP8X4),
                lhsT_scale=h_scales[b],
                rhs=vw[first][:].bitcast(FP8X4),
                rhs_scale=vs[:, first:last],
                start=True,
                stop=True,
            )

        def finish(a, b):
            if (a, b) == (0, 0):
                pair.append(keep.tile([P, 2, nv], F32, align_bytes=256, name="best_pair"))
            joint = a == 0 and b < 2
            best = pair[0][:, b] if joint else keep.tile([P, nv], F32, align_bytes=256, name="best%d_%d" % (a, b))[:]
            odd = late.tile([P, nv], F32, align_bytes=64, name="odd%d_%d" % (a, b), offset=16384 + (a * blocks + b) * 1024)
            nc.scalar.copy(odd[:], y_acc[a, b][:, 1::2])
            nc.vector.tensor_tensor(best, y_acc[a, b][:, 0::2], odd[:], MAX)
            if not joint:
                nc.sync.dma_start(out=out[b * P : (b + 1) * P, a * nv : (a + 1) * nv], in_=best)
            elif b == 1:
                nc.sync.dma_start(out=out[: 2 * P, :nv].rearrange("(b p) v -> p b v", b=2), in_=pair[0][:])

        for b in range(blocks):
            project(b)
        gather_docs(0, 512, 36864)
        quantise_h(0, 2, 2048)
        for b in range(2):
            score(b, 0, 512)
        gather_docs(512, 768, 1024)
        for b in range(2):
            score(b, 512, 768)
        quantise_h(2, 3, 2304)
        score(2, 0, 512)
        score(2, 512, 768)
        gather_docs(768, 1024, 2560)
        for b in range(3):
            score(b, 768, 1024)
        finish(0, 0)
        finish(0, 1)
        quantise_h(3, 4, 16384)
        score(3, 0, 512)
        score(3, 512, 768)
        score(3, 768, 1024)
        for a, b in ((0, 2), (1, 0), (1, 1), (1, 2), (0, 3), (1, 3)):
            finish(a, b)
